import numpy as np
import ml_dtypes


def mxq(x, axis, fmt="e4m3"):
    dtype, down = {"e4m3": (ml_dtypes.float8_e4m3fn, 7), "e5m2": (ml_dtypes.float8_e5m2, 14)}[fmt]
    v = np.moveaxis(np.asarray(x, np.float32).astype(ml_dtypes.bfloat16).astype(np.float64), axis, -1)
    blocks = v.reshape(v.shape[:-1] + (-1, 32))
    amax = np.abs(blocks).max(-1, keepdims=True)
    byte = np.maximum(np.where(amax > 0, np.frexp(amax)[1] - 1 + 127, 0) - down, 1)
    scale = np.exp2(byte - 127.0)
    codes = (blocks / scale).astype(np.float32).astype(dtype).astype(np.float64)
    return np.moveaxis((codes * scale).reshape(v.shape), -1, axis)


WIDE = False


def mx_kscale(k):
    if not WIDE:
        return np.ones(k)
    levels = np.array([10, -10, 5, -5, 0])
    if k % 512:
        return np.exp2(np.random.permutation(np.resize(levels, k // 32))).repeat(32)
    a = np.empty((k // 512, 16))
    for p in range(k // 512):
        a[p, :8] = np.random.permutation(np.resize(levels, 8))
        for g in range(8):
            far = levels[np.abs(levels - a[p, g]) >= 10]
            a[p, g + 8] = far[np.random.randint(len(far))]
    return np.exp2(a.ravel()).repeat(32)


def f64(x):
    return np.asarray(x).astype(np.float64)


def striped(idx):
    return np.tile(idx.reshape(-1, 16).T, (8, 1)).astype(np.uint16)


def unstriped(offs):
    return offs[:16].T.reshape(-1).astype(np.int64)


def pack_weight(w):
    k, n = w.shape
    w = f64(np.asarray(w, np.float32).astype(ml_dtypes.bfloat16)).reshape(k // 32, 32, n)
    amax = np.abs(w).max(1)
    byte = np.clip(np.where(amax > 0, np.frexp(amax)[1] - 1 + 127 - 7, 1), 1, 254)
    scaled = (w * np.exp2(127.0 - byte)[:, None, :]).reshape(k, n).astype(np.float32)
    words = np.ascontiguousarray(scaled.reshape(k // 512, 128, 4, n).transpose(0, 1, 3, 2)).astype(ml_dtypes.float8_e4m3fn).view(np.uint8)
    return words, np.ascontiguousarray(byte.astype(np.uint8).reshape(k // 512, 16, n))


def unpack_weight(words, scales):
    g, p, n, _ = words.shape
    vals = np.ascontiguousarray(words).view(ml_dtypes.float8_e4m3fn).astype(np.float64) * np.repeat(np.exp2(scales.astype(np.float64) - 127.0), 8, axis=1)[..., None]
    return vals.transpose(0, 1, 3, 2).reshape(g * 512, n)


def relu(v):
    return np.maximum(v, 0.0)


K, T, D, S, V, N = 512, 1024, 2, 512, 256, 256


def setup_inputs():
    n = np.random.standard_normal
    s = mx_kscale(K)[:, None]
    words, scales = pack_weight(n((K, N)) / np.sqrt(K) / s)
    return {
        "xT": (n((K, T)) * s).astype(np.float32),
        "w_words": words,
        "w_scales": scales,
        "b": (0.3 * n((N, 1))).astype(np.float32),
        "gate": np.tile(np.random.uniform(0.2, 1.0, (D, 1, V)) / np.sqrt(D), (1, N, 1)).astype(np.float32),
        "offs": striped(np.random.permutation(T)[:S]),
        "pos1": striped(np.random.permutation(S)[:V]),
        "pos2": striped(np.random.permutation(S)[:V]),
    }


def reference(xT, w_words, w_scales, b, gate, offs, pos1, pos2):
    w = unpack_weight(w_words, w_scales)
    idx = unstriped(offs)
    xq = mxq(f64(xT)[:, idx], 0, "e4m3")
    y = w.T @ xq
    y = relu(y + f64(b))
    return sum(f64(gate[d]) * y[:, unstriped(p)] for d, p in enumerate((pos1, pos2)))

@@ -1,0 +1,112 @@
+from contextlib import ExitStack
+
+import concourse.mybir as mybir
+
+K, T, S, V, N, D = 512, 1024, 512, 256, 256, 2
+FLOPS = 2 * K * N * S
+
+F32 = mybir.dt.float32
+BF16 = mybir.dt.bfloat16
+I32 = mybir.dt.int32
+U32 = mybir.dt.uint32
+U16 = mybir.dt.uint16
+U8 = mybir.dt.uint8
+FP8X4 = mybir.dt.float8_e4m3fn_x4
+RELU = mybir.ActivationFunctionType.Relu
+MULT = mybir.AluOpType.mult
+ADD = mybir.AluOpType.add
+
+P = 128
+PACK = 4
+HALVES = N // P
+QUARTER = S // 4
+PIECES = ((0, 256), (256, 384), (384, 512))
+
+
+def tile_picked_sub_lin_relu_sub_e_kernel(tc, xT, w_words, w_scales, b, gate, offs, pos1, pos2, out):
+    nc = tc.nc
+    with ExitStack() as ctx:
+        keep = ctx.enter_context(tc.tile_pool(name="keep", bufs=1))
+        psum = ctx.enter_context(tc.psum_pool(name="psum", bufs=1))
+
+        offs_sb = keep.tile([P, S // 16], U16, name="offs_sb")
+        pos_sb = [keep.tile([P, V // 16], U16, name=f"pos_sb{d}") for d in range(D)]
+        planes = [keep.tile([P, T], F32, name=f"plane{j}", align_bytes=64) for j in range(PACK)]
+        w_codes = keep.tile([P, N], U32, name="w_codes", align_bytes=64)
+        w_scale = keep.tile([P, N], U8, name="w_scale", align_bytes=64)
+        bias = keep.tile([P, HALVES, 8], F32, name="bias")
+        gate_sb = keep.tile([P, D * HALVES, V], F32, name="gate_sb", align_bytes=64)
+        warm = keep.tile([P, 16], F32, name="warm")
+
+        nc.vector.memset(warm[:, 0:8], 0.0)
+        nc.vector.memset(w_scale[:].bitcast(I32), 0)
+        nc.scalar.activation(warm[:, 8:16], warm[:, 0:8], RELU)
+
+        x_rows = xT.rearrange("(p j) t -> p j t", j=PACK)
+        nc.sync.dma_start(offs_sb[:], offs)
+        for j in range(PACK):
+            nc.sync.dma_start(planes[j][:], x_rows[:, j, :])
+        nc.sync.dma_start(w_codes[:].bitcast(I32), w_words[0].rearrange("p n r -> p (n r)").bitcast(I32))
+        for quadrant in range(4):
+            nc.sync.dma_start(
+                w_scale[32 * quadrant : 32 * quadrant + 4, :].bitcast(I32),
+                w_scales[0, 4 * quadrant : 4 * quadrant + 4, :].bitcast(I32),
+            )
+        with nc.allow_non_contiguous_dma(reason="one bias value a partition"):
+            nc.sync.dma_start(bias[:, :, 0:1], b.rearrange("(h p) o -> p h o", p=P))
+        nc.sync.dma_start(gate_sb[:], gate.rearrange("d (h p) v -> p (d h) v", p=P))
+        nc.sync.dma_start(pos_sb[0][:], pos1)
+        nc.sync.dma_start(pos_sb[1][:], pos2)
+
+        pairs = keep.tile([P, 2, S, 2], BF16, name="pairs", align_bytes=64)
+        for j in range(PACK - 1):
+            nc.vector.tensor_copy(pairs[:, j // 2, :, j % 2], planes[j][:].indirect(offs_sb[:]))
+        quads = keep.tile([P, S, 2, 2], BF16, name="quads", align_bytes=64)
+        for c in range(4):
+            lo, hi = c * QUARTER, (c + 1) * QUARTER
+            nc.vector.tensor_copy(pairs[:, 1, lo:hi, 1], planes[3][:].indirect(offs_sb[:, lo // 16 : hi // 16]))
+            nc.scalar.copy(quads[:, lo:hi, :, :], pairs[:, :, lo:hi, :].rearrange("p u n e -> p n u e"))
+
+        x_codes = keep.tile([P, S], U32, name="x_codes", align_bytes=64)
+        x_scale = keep.tile([P, S], U8, name="x_scale", align_bytes=64)
+        banks = [[psum.tile([P, S // 2], F32, name=f"bank{h}{c}") for c in range(2)] for h in range(HALVES)]
+        for lo, hi in PIECES:
+            nc.vector.quantize_mx(
+                out=x_codes[:, lo:hi].bitcast(FP8X4),
+                scales=x_scale[:, lo:hi],
+                in_=quads[:, lo:hi, :, :].rearrange("p n u e -> p (n u e)"),
+            )
+            for h in range(HALVES):
+                c = lo // (S // 2)
+                nc.tensor.matmul_mx(
+                    out=banks[h][c][:, lo - c * (S // 2) : hi - c * (S // 2)],
+                    lhsT=w_codes[:, h * P : (h + 1) * P].bitcast(FP8X4),
+                    lhsT_scale=w_scale[:, h * P : (h + 1) * P],
+                    rhs=x_codes[:, lo:hi].bitcast(FP8X4),
+                    rhs_scale=x_scale[:, lo:hi],
+                    start=True,
+                    stop=True,
+                )
+
+        y = [keep.tile([P, S], F32, name=f"y{h}", align_bytes=64) for h in range(HALVES)]
+        for h in range(HALVES):
+            for c in range(2):
+                nc.scalar.activation(y[h][:, c * (S // 2) : (c + 1) * (S // 2)], banks[h][c][:], RELU, bias=bias[:, h, 0:1])
+
+        terms = keep.tile([P, D * HALVES, V], F32, name="terms", align_bytes=64)
+        total = [keep.tile([P, V], F32, name=f"total{h}", align_bytes=64) for h in range(HALVES)]
+
+        def fetch(h, d):
+            slot = d * HALVES + h
+            nc.vector.tensor_tensor(terms[:, slot, :], y[h][:].indirect(pos_sb[d][:]), gate_sb[:, slot, :], MULT)
+
+        def finish(h):
+            nc.vector.tensor_tensor(total[h][:], terms[:, h, :], terms[:, HALVES + h, :], ADD)
+            nc.sync.dma_start(out[h * P : (h + 1) * P, :], total[h][:])
+
+        fetch(0, 0)
+        fetch(0, 1)
+        fetch(1, 0)
+        finish(0)
+        fetch(1, 1)
+        finish(1)

@@ -62,10 +62,12 @@ def tile_picked_sub_lin_relu_sub_e_kernel(tc, xT, w_words, w_scales, b, gate, of
         for j in range(PACK - 1):
             nc.vector.tensor_copy(pairs[:, j // 2, :, j % 2], planes[j][:].indirect(offs_sb[:]))
         quads = keep.tile([P, S, 2, 2], BF16, name="quads", align_bytes=64)
+        pair_words = pairs[:].rearrange("p u n e -> p (u n e)").bitcast(F32).rearrange("p (u n) -> p u n", u=2)
+        quad_words = quads[:].rearrange("p n u e -> p (n u e)").bitcast(F32).rearrange("p (n u) -> p n u", u=2)
         for c in range(4):
             lo, hi = c * QUARTER, (c + 1) * QUARTER
             nc.vector.tensor_copy(pairs[:, 1, lo:hi, 1], planes[3][:].indirect(offs_sb[:, lo // 16 : hi // 16]))
-            nc.scalar.copy(quads[:, lo:hi, :, :], pairs[:, :, lo:hi, :].rearrange("p u n e -> p n u e"))
+            nc.scalar.copy(quad_words[:, lo:hi, :], pair_words[:, :, lo:hi].rearrange("p u n -> p n u"))
 
         x_codes = keep.tile([P, S], U32, name="x_codes", align_bytes=64)
         x_scale = keep.tile([P, S], U8, name="x_scale", align_bytes=64)

@@ -35,7 +35,7 @@ def tile_picked_sub_lin_relu_sub_e_kernel(tc, xT, w_words, w_scales, b, gate, of
         w_codes = keep.tile([P, N], U32, name="w_codes", align_bytes=64)
         w_scale = keep.tile([P, N], U8, name="w_scale", align_bytes=64)
         bias = keep.tile([P, HALVES, 8], F32, name="bias")
-        gate_sb = keep.tile([P, D * HALVES, V], F32, name="gate_sb", align_bytes=64)
+        gate_sb = keep.tile([P, D, V], F32, name="gate_sb", align_bytes=64)
         warm = keep.tile([P, 16], F32, name="warm")
 
         nc.vector.memset(warm[:, 0:8], 0.0)
@@ -43,20 +43,30 @@ def tile_picked_sub_lin_relu_sub_e_kernel(tc, xT, w_words, w_scales, b, gate, of
         nc.scalar.activation(warm[:, 8:16], warm[:, 0:8], RELU)
 
         x_rows = xT.rearrange("(p j) t -> p j t", j=PACK)
-        nc.sync.dma_start(offs_sb[:], offs)
-        for j in range(PACK):
+        def load_plane(j):
             nc.sync.dma_start(planes[j][:], x_rows[:, j, :])
-        nc.sync.dma_start(w_codes[:].bitcast(I32), w_words[0].rearrange("p n r -> p (n r)").bitcast(I32))
-        for quadrant in range(4):
+
+        def load_scales(quadrant):
             nc.sync.dma_start(
                 w_scale[32 * quadrant : 32 * quadrant + 4, :].bitcast(I32),
                 w_scales[0, 4 * quadrant : 4 * quadrant + 4, :].bitcast(I32),
             )
+
+        nc.sync.dma_start(offs_sb[:], offs)
+        load_plane(0)
+        load_plane(1)
+        load_scales(0)
+        load_scales(1)
+        load_plane(2)
+        load_scales(2)
+        load_scales(3)
+        load_plane(3)
+        nc.sync.dma_start(w_codes[:].bitcast(I32), w_words[0].rearrange("p n r -> p (n r)").bitcast(I32))
         with nc.allow_non_contiguous_dma(reason="one bias value a partition"):
             nc.sync.dma_start(bias[:, :, 0:1], b.rearrange("(h p) o -> p h o", p=P))
-        nc.sync.dma_start(gate_sb[:], gate.rearrange("d (h p) v -> p (d h) v", p=P))
         nc.sync.dma_start(pos_sb[0][:], pos1)
         nc.sync.dma_start(pos_sb[1][:], pos2)
+        nc.sync.dma_start(gate_sb[:], gate[:, 0:P, :].rearrange("d p v -> p d v"))
 
         pairs = keep.tile([P, 2, S, 2], BF16, name="pairs", align_bytes=64)
         for j in range(PACK - 1):
@@ -100,7 +110,7 @@ def tile_picked_sub_lin_relu_sub_e_kernel(tc, xT, w_words, w_scales, b, gate, of
 
         def fetch(h, d):
             slot = d * HALVES + h
-            nc.vector.tensor_tensor(terms[:, slot, :], y[h][:].indirect(pos_sb[d][:]), gate_sb[:, slot, :], MULT)
+            nc.vector.tensor_tensor(terms[:, slot, :], y[h][:].indirect(pos_sb[d][:]), gate_sb[:, d, :], MULT)
 
         def finish(h):
             nc.vector.tensor_tensor(total[h][:], terms[:, h, :], terms[:, HALVES + h, :], ADD)

@@ -15,12 +15,12 @@ FP8X4 = mybir.dt.float8_e4m3fn_x4
 RELU = mybir.ActivationFunctionType.Relu
 MULT = mybir.AluOpType.mult
 ADD = mybir.AluOpType.add
+MAX = mybir.AluOpType.max
 
 P = 128
 PACK = 4
 HALVES = N // P
 QUARTER = S // 4
-PIECES = ((0, 256), (256, 384), (384, 512))
 
 
 def tile_picked_sub_lin_relu_sub_e_kernel(tc, xT, w_words, w_scales, b, gate, offs, pos1, pos2, out):
@@ -81,29 +81,43 @@ def tile_picked_sub_lin_relu_sub_e_kernel(tc, xT, w_words, w_scales, b, gate, of
 
         x_codes = keep.tile([P, S], U32, name="x_codes", align_bytes=64)
         x_scale = keep.tile([P, S], U8, name="x_scale", align_bytes=64)
-        banks = [[psum.tile([P, S // 2], F32, name=f"bank{h}{c}") for c in range(2)] for h in range(HALVES)]
-        for lo, hi in PIECES:
+        y = [keep.tile([P, S], F32, name=f"y{h}", align_bytes=64) for h in range(HALVES)]
+
+        def quantise(lo, hi):
             nc.vector.quantize_mx(
                 out=x_codes[:, lo:hi].bitcast(FP8X4),
                 scales=x_scale[:, lo:hi],
                 in_=quads[:, lo:hi, :, :].rearrange("p n u e -> p (n u e)"),
             )
-            for h in range(HALVES):
-                c = lo // (S // 2)
-                nc.tensor.matmul_mx(
-                    out=banks[h][c][:, lo - c * (S // 2) : hi - c * (S // 2)],
-                    lhsT=w_codes[:, h * P : (h + 1) * P].bitcast(FP8X4),
-                    lhsT_scale=w_scale[:, h * P : (h + 1) * P],
-                    rhs=x_codes[:, lo:hi].bitcast(FP8X4),
-                    rhs_scale=x_scale[:, lo:hi],
-                    start=True,
-                    stop=True,
-                )
 
-        y = [keep.tile([P, S], F32, name=f"y{h}", align_bytes=64) for h in range(HALVES)]
-        for h in range(HALVES):
-            for c in range(2):
-                nc.scalar.activation(y[h][:, c * (S // 2) : (c + 1) * (S // 2)], banks[h][c][:], RELU, bias=bias[:, h, 0:1])
+        def multiply(h, lo, hi, target):
+            nc.tensor.matmul_mx(
+                out=target,
+                lhsT=w_codes[:, h * P : (h + 1) * P].bitcast(FP8X4),
+                lhsT_scale=w_scale[:, h * P : (h + 1) * P],
+                rhs=x_codes[:, lo:hi].bitcast(FP8X4),
+                rhs_scale=x_scale[:, lo:hi],
+                start=True,
+                stop=True,
+            )
+
+        def rectify(h, lo, hi, bank):
+            nc.scalar.activation(y[h][:, lo:hi], bank, RELU, bias=bias[:, h, 0:1])
+
+        early = psum.tile([P, 2 * QUARTER], F32, name="early")
+        third = psum.tile([P, QUARTER], F32, name="third")
+        last = psum.tile([P, QUARTER], F32, name="last")
+        targets = (early[:, 0:QUARTER], early[:, QUARTER:], third[:], last[:])
+        for c in range(4):
+            quantise(c * QUARTER, (c + 1) * QUARTER)
+            multiply(0, c * QUARTER, (c + 1) * QUARTER, targets[c])
+        rectify(0, 0, 2 * QUARTER, early[:])
+        rectify(0, 2 * QUARTER, 3 * QUARTER, third[:])
+        nc.vector.tensor_scalar(y[0][:, 3 * QUARTER :], last[:], bias[:, 0, 0:1], 0.0, ADD, MAX)
+        for c in range(2):
+            bank = psum.tile([P, S // 2], F32, name=f"second{c}")
+            multiply(1, c * (S // 2), (c + 1) * (S // 2), bank[:])
+            rectify(1, c * (S // 2), (c + 1) * (S // 2), bank[:])
 
         terms = keep.tile([P, D * HALVES, V], F32, name="terms", align_bytes=64)
         total = [keep.tile([P, V], F32, name=f"total{h}", align_bytes=64) for h in range(HALVES)]

@@ -52,16 +52,13 @@ def tile_picked_sub_lin_relu_sub_e_kernel(tc, xT, w_words, w_scales, b, gate, of
                 w_scales[0, 4 * quadrant : 4 * quadrant + 4, :].bitcast(I32),
             )
 
-        nc.sync.dma_start(offs_sb[:], offs)
         load_plane(0)
-        load_plane(1)
-        load_scales(0)
-        load_scales(1)
-        load_plane(2)
-        load_scales(2)
-        load_scales(3)
-        load_plane(3)
+        nc.sync.dma_start(offs_sb[:], offs)
+        for j in range(1, PACK):
+            load_plane(j)
         nc.sync.dma_start(w_codes[:].bitcast(I32), w_words[0].rearrange("p n r -> p (n r)").bitcast(I32))
+        for quadrant in range(4):
+            load_scales(quadrant)
         with nc.allow_non_contiguous_dma(reason="one bias value a partition"):
             nc.sync.dma_start(bias[:, :, 0:1], b.rearrange("(h p) o -> p h o", p=P))
         nc.sync.dma_start(pos_sb[0][:], pos1)

@@ -125,11 +125,12 @@ def tile_picked_sub_lin_relu_sub_e_kernel(tc, xT, w_words, w_scales, b, gate, of
 
         def finish(h):
             nc.vector.tensor_tensor(total[h][:], terms[:, h, :], terms[:, HALVES + h, :], ADD)
-            nc.sync.dma_start(out[h * P : (h + 1) * P, :], total[h][:])
+            queue = nc.scalar if h == 0 else nc.sync
+            queue.dma_start(out[h * P : (h + 1) * P, :], total[h][:])
 
         fetch(0, 0)
         fetch(0, 1)
         fetch(1, 0)
-        finish(0)
         fetch(1, 1)
+        finish(0)
         finish(1)

@@ -31,11 +31,10 @@ def tile_picked_sub_lin_relu_sub_e_kernel(tc, xT, w_words, w_scales, b, gate, of
 
         offs_sb = keep.tile([P, S // 16], U16, name="offs_sb")
         pos_sb = [keep.tile([P, V // 16], U16, name=f"pos_sb{d}") for d in range(D)]
-        planes = [keep.tile([P, T], F32, name=f"plane{j}", align_bytes=64) for j in range(PACK)]
+        planes = [keep.tile([P, T], F32, name=f"plane{j}", tag=f"plane{j}", align_bytes=64) for j in range(PACK)]
         w_codes = keep.tile([P, N], U32, name="w_codes", align_bytes=64)
         w_scale = keep.tile([P, N], U8, name="w_scale", align_bytes=64)
         bias = keep.tile([P, HALVES, 8], F32, name="bias")
-        gate_sb = keep.tile([P, D, V], F32, name="gate_sb", align_bytes=64)
         warm = keep.tile([P, 16], F32, name="warm")
 
         nc.vector.memset(warm[:, 0:8], 0.0)
@@ -63,11 +62,12 @@ def tile_picked_sub_lin_relu_sub_e_kernel(tc, xT, w_words, w_scales, b, gate, of
             nc.sync.dma_start(bias[:, :, 0:1], b.rearrange("(h p) o -> p h o", p=P))
         nc.sync.dma_start(pos_sb[0][:], pos1)
         nc.sync.dma_start(pos_sb[1][:], pos2)
-        nc.sync.dma_start(gate_sb[:], gate[:, 0:P, :].rearrange("d p v -> p d v"))
 
         pairs = keep.tile([P, 2, S, 2], BF16, name="pairs", align_bytes=64)
         for j in range(PACK - 1):
             nc.vector.tensor_copy(pairs[:, j // 2, :, j % 2], planes[j][:].indirect(offs_sb[:]))
+        gate_sb = keep.tile([P, D, V], F32, name="gate_sb", tag="plane1", align_bytes=64)
+        nc.scalar.dma_start(gate_sb[:], gate[:, 0:P, :].rearrange("d p v -> p d v"))
         quads = keep.tile([P, S, 2, 2], BF16, name="quads", align_bytes=64)
         pair_words = pairs[:].rearrange("p u n e -> p (u n e)").bitcast(F32).rearrange("p (u n) -> p u n", u=2)
         quad_words = quads[:].rearrange("p n u e -> p (n u e)").bitcast(F32).rearrange("p (n u) -> p n u", u=2)

@@ -66,7 +66,7 @@ def tile_picked_sub_lin_relu_sub_e_kernel(tc, xT, w_words, w_scales, b, gate, of
         pairs = keep.tile([P, 2, S, 2], BF16, name="pairs", align_bytes=64)
         for j in range(PACK - 1):
             nc.vector.tensor_copy(pairs[:, j // 2, :, j % 2], planes[j][:].indirect(offs_sb[:]))
-        gate_sb = keep.tile([P, D, V], F32, name="gate_sb", tag="plane1", align_bytes=64)
+        gate_sb = keep.tile([P, D, V], F32, name="gate_sb", tag="plane2", align_bytes=64)
         nc.scalar.dma_start(gate_sb[:], gate[:, 0:P, :].rearrange("d p v -> p d v"))
         quads = keep.tile([P, S, 2, 2], BF16, name="quads", align_bytes=64)
         pair_words = pairs[:].rearrange("p u n e -> p (u n e)").bitcast(F32).rearrange("p (u n) -> p u n", u=2)

@@ -15,7 +15,6 @@ FP8X4 = mybir.dt.float8_e4m3fn_x4
 RELU = mybir.ActivationFunctionType.Relu
 MULT = mybir.AluOpType.mult
 ADD = mybir.AluOpType.add
-MAX = mybir.AluOpType.max
 
 P = 128
 PACK = 4
@@ -110,7 +109,7 @@ def tile_picked_sub_lin_relu_sub_e_kernel(tc, xT, w_words, w_scales, b, gate, of
             multiply(0, c * QUARTER, (c + 1) * QUARTER, targets[c])
         rectify(0, 0, 2 * QUARTER, early[:])
         rectify(0, 2 * QUARTER, 3 * QUARTER, third[:])
-        nc.vector.tensor_scalar(y[0][:, 3 * QUARTER :], last[:], bias[:, 0, 0:1], 0.0, ADD, MAX)
+        rectify(0, 3 * QUARTER, S, last[:])
         for c in range(2):
             bank = psum.tile([P, S // 2], F32, name=f"second{c}")
             multiply(1, c * (S // 2), (c + 1) * (S // 2), bank[:])

@@ -63,6 +63,7 @@ def tile_picked_sub_lin_relu_sub_e_kernel(tc, xT, w_words, w_scales, b, gate, of
         nc.sync.dma_start(pos_sb[1][:], pos2)
 
         pairs = keep.tile([P, 2, S, 2], BF16, name="pairs", align_bytes=64)
+        nc.vector.memset(pairs[:, 1, 3 * QUARTER :, :], 0.0)
         for j in range(PACK - 1):
             nc.vector.tensor_copy(pairs[:, j // 2, :, j % 2], planes[j][:].indirect(offs_sb[:]))
         gate_sb = keep.tile([P, D, V], F32, name="gate_sb", tag="plane2", align_bytes=64)
@@ -70,10 +71,16 @@ def tile_picked_sub_lin_relu_sub_e_kernel(tc, xT, w_words, w_scales, b, gate, of
         quads = keep.tile([P, S, 2, 2], BF16, name="quads", align_bytes=64)
         pair_words = pairs[:].rearrange("p u n e -> p (u n e)").bitcast(F32).rearrange("p (u n) -> p u n", u=2)
         quad_words = quads[:].rearrange("p n u e -> p (n u e)").bitcast(F32).rearrange("p (n u) -> p n u", u=2)
-        for c in range(4):
+
+        def weave(lo, hi):
+            nc.scalar.copy(quad_words[:, lo:hi, :], pair_words[:, :, lo:hi].rearrange("p u n -> p n u"))
+
+        weave(3 * QUARTER, S)
+        for c in range(3):
             lo, hi = c * QUARTER, (c + 1) * QUARTER
             nc.vector.tensor_copy(pairs[:, 1, lo:hi, 1], planes[3][:].indirect(offs_sb[:, lo // 16 : hi // 16]))
-            nc.scalar.copy(quad_words[:, lo:hi, :], pair_words[:, :, lo:hi].rearrange("p u n -> p n u"))
+            weave(lo, hi)
+        nc.vector.tensor_copy(quads[:, 3 * QUARTER :, 1, 1], planes[3][:].indirect(offs_sb[:, 3 * QUARTER // 16 :]))
 
         x_codes = keep.tile([P, S], U32, name="x_codes", align_bytes=64)
         x_scale = keep.tile([P, S], U8, name="x_scale", align_bytes=64)

@@ -62,35 +62,40 @@ def tile_picked_sub_lin_relu_sub_e_kernel(tc, xT, w_words, w_scales, b, gate, of
         nc.sync.dma_start(pos_sb[0][:], pos1)
         nc.sync.dma_start(pos_sb[1][:], pos2)
 
-        pairs = keep.tile([P, 2, S, 2], BF16, name="pairs", align_bytes=64)
+        pairs = keep.tile([P, 2, S, 2], BF16, name="pairs", tag="pairs", align_bytes=64)
         nc.vector.memset(pairs[:, 1, 3 * QUARTER :, :], 0.0)
         for j in range(PACK - 1):
             nc.vector.tensor_copy(pairs[:, j // 2, :, j % 2], planes[j][:].indirect(offs_sb[:]))
         gate_sb = keep.tile([P, D, V], F32, name="gate_sb", tag="plane2", align_bytes=64)
         nc.scalar.dma_start(gate_sb[:], gate[:, 0:P, :].rearrange("d p v -> p d v"))
-        quads = keep.tile([P, S, 2, 2], BF16, name="quads", align_bytes=64)
+        quads = [keep.tile([P, QUARTER, 2, 2], BF16, name=f"quads{c}", align_bytes=64) for c in range(4)]
         pair_words = pairs[:].rearrange("p u n e -> p (u n e)").bitcast(F32).rearrange("p (u n) -> p u n", u=2)
-        quad_words = quads[:].rearrange("p n u e -> p (n u e)").bitcast(F32).rearrange("p (n u) -> p n u", u=2)
 
-        def weave(lo, hi):
-            nc.scalar.copy(quad_words[:, lo:hi, :], pair_words[:, :, lo:hi].rearrange("p u n -> p n u"))
+        def weave(c):
+            words = quads[c][:].rearrange("p n u e -> p (n u e)").bitcast(F32).rearrange("p (n u) -> p n u", u=2)
+            nc.scalar.copy(words, pair_words[:, :, c * QUARTER : (c + 1) * QUARTER].rearrange("p u n -> p n u"))
 
-        weave(3 * QUARTER, S)
+        weave(3)
         for c in range(3):
             lo, hi = c * QUARTER, (c + 1) * QUARTER
             nc.vector.tensor_copy(pairs[:, 1, lo:hi, 1], planes[3][:].indirect(offs_sb[:, lo // 16 : hi // 16]))
-            weave(lo, hi)
-        nc.vector.tensor_copy(quads[:, 3 * QUARTER :, 1, 1], planes[3][:].indirect(offs_sb[:, 3 * QUARTER // 16 :]))
+            weave(c)
+        nc.vector.tensor_copy(quads[3][:, :, 1, 1], planes[3][:].indirect(offs_sb[:, 3 * QUARTER // 16 :]))
 
-        x_codes = keep.tile([P, S], U32, name="x_codes", align_bytes=64)
+        x_codes = keep.tile([P, 3 * QUARTER], U32, name="x_codes", align_bytes=64)
+        last_codes = keep.tile([P, QUARTER], U32, name="last_codes", tag="pairs", align_bytes=64)
+
+        def codes(lo, hi):
+            return last_codes[:] if lo == 3 * QUARTER else x_codes[:, lo:hi]
+
         x_scale = keep.tile([P, S], U8, name="x_scale", align_bytes=64)
         y = [keep.tile([P, S], F32, name=f"y{h}", align_bytes=64) for h in range(HALVES)]
 
         def quantise(lo, hi):
             nc.vector.quantize_mx(
-                out=x_codes[:, lo:hi].bitcast(FP8X4),
+                out=codes(lo, hi).bitcast(FP8X4),
                 scales=x_scale[:, lo:hi],
-                in_=quads[:, lo:hi, :, :].rearrange("p n u e -> p (n u e)"),
+                in_=quads[lo // QUARTER][:].rearrange("p n u e -> p (n u e)"),
             )
 
         def multiply(h, lo, hi, target):
@@ -98,7 +103,7 @@ def tile_picked_sub_lin_relu_sub_e_kernel(tc, xT, w_words, w_scales, b, gate, of
                 out=target,
                 lhsT=w_codes[:, h * P : (h + 1) * P].bitcast(FP8X4),
                 lhsT_scale=w_scale[:, h * P : (h + 1) * P],
-                rhs=x_codes[:, lo:hi].bitcast(FP8X4),
+                rhs=codes(lo, hi).bitcast(FP8X4),
                 rhs_scale=x_scale[:, lo:hi],
                 start=True,
                 stop=True,
@@ -117,10 +122,13 @@ def tile_picked_sub_lin_relu_sub_e_kernel(tc, xT, w_words, w_scales, b, gate, of
         rectify(0, 0, 2 * QUARTER, early[:])
         rectify(0, 2 * QUARTER, 3 * QUARTER, third[:])
         rectify(0, 3 * QUARTER, S, last[:])
-        for c in range(2):
-            bank = psum.tile([P, S // 2], F32, name=f"second{c}")
-            multiply(1, c * (S // 2), (c + 1) * (S // 2), bank[:])
-            rectify(1, c * (S // 2), (c + 1) * (S // 2), bank[:])
+        front = psum.tile([P, 2 * QUARTER], F32, name="front")
+        multiply(1, 0, 2 * QUARTER, front[:])
+        rectify(1, 0, 2 * QUARTER, front[:])
+        back = psum.tile([P, 2 * QUARTER], F32, name="back")
+        multiply(1, 2 * QUARTER, 3 * QUARTER, back[:, 0:QUARTER])
+        multiply(1, 3 * QUARTER, S, back[:, QUARTER:])
+        rectify(1, 2 * QUARTER, S, back[:])
 
         terms = keep.tile([P, D * HALVES, V], F32, name="terms", align_bytes=64)
         total = [keep.tile([P, V], F32, name=f"total{h}", align_bytes=64) for h in range(HALVES)]

@@ -13,6 +13,7 @@ U16 = mybir.dt.uint16
 U8 = mybir.dt.uint8
 FP8X4 = mybir.dt.float8_e4m3fn_x4
 RELU = mybir.ActivationFunctionType.Relu
+COPY = mybir.ActivationFunctionType.Copy
 MULT = mybir.AluOpType.mult
 ADD = mybir.AluOpType.add
 
@@ -64,8 +65,11 @@ def tile_picked_sub_lin_relu_sub_e_kernel(tc, xT, w_words, w_scales, b, gate, of
 
         pairs = keep.tile([P, 2, S, 2], BF16, name="pairs", tag="pairs", align_bytes=64)
         nc.vector.memset(pairs[:, 1, 3 * QUARTER :, :], 0.0)
-        for j in range(PACK - 1):
-            nc.vector.tensor_copy(pairs[:, j // 2, :, j % 2], planes[j][:].indirect(offs_sb[:]))
+        for j in range(2):
+            rounded = keep.tile([P, T], BF16, name=f"rounded{j}", align_bytes=64)
+            nc.vector.tensor_copy(rounded[:], planes[j][:])
+            nc.scalar.activation(pairs[:, 0, :, j], rounded[:].indirect(offs_sb[:]), COPY)
+        nc.vector.tensor_copy(pairs[:, 1, :, 0], planes[2][:].indirect(offs_sb[:]))
         gate_sb = keep.tile([P, D, V], F32, name="gate_sb", tag="plane2", align_bytes=64)
         nc.scalar.dma_start(gate_sb[:], gate[:, 0:P, :].rearrange("d p v -> p d v"))
         quads = [keep.tile([P, QUARTER, 2, 2], BF16, name=f"quads{c}", align_bytes=64) for c in range(4)]
@@ -112,16 +116,12 @@ def tile_picked_sub_lin_relu_sub_e_kernel(tc, xT, w_words, w_scales, b, gate, of
         def rectify(h, lo, hi, bank):
             nc.scalar.activation(y[h][:, lo:hi], bank, RELU, bias=bias[:, h, 0:1])
 
-        early = psum.tile([P, 2 * QUARTER], F32, name="early")
-        third = psum.tile([P, QUARTER], F32, name="third")
-        last = psum.tile([P, QUARTER], F32, name="last")
-        targets = (early[:, 0:QUARTER], early[:, QUARTER:], third[:], last[:])
         for c in range(4):
-            quantise(c * QUARTER, (c + 1) * QUARTER)
-            multiply(0, c * QUARTER, (c + 1) * QUARTER, targets[c])
-        rectify(0, 0, 2 * QUARTER, early[:])
-        rectify(0, 2 * QUARTER, 3 * QUARTER, third[:])
-        rectify(0, 3 * QUARTER, S, last[:])
+            lo, hi = c * QUARTER, (c + 1) * QUARTER
+            bank = psum.tile([P, QUARTER], F32, name=f"first{c}")
+            quantise(lo, hi)
+            multiply(0, lo, hi, bank[:])
+            rectify(0, lo, hi, bank[:])
         front = psum.tile([P, 2 * QUARTER], F32, name="front")
         multiply(1, 0, 2 * QUARTER, front[:])
         rectify(1, 0, 2 * QUARTER, front[:])

@@ -66,11 +66,11 @@ def tile_picked_sub_lin_relu_sub_e_kernel(tc, xT, w_words, w_scales, b, gate, of
         pairs = keep.tile([P, 2, S, 2], BF16, name="pairs", tag="pairs", align_bytes=64)
         nc.vector.memset(pairs[:, 1, 3 * QUARTER :, :], 0.0)
         for j in range(2):
-            rounded = keep.tile([P, T], BF16, name=f"rounded{j}", align_bytes=64)
+            rounded = keep.tile([P, T], BF16, name=f"rounded{j}", tag=f"rounded{j}", align_bytes=64)
             nc.vector.tensor_copy(rounded[:], planes[j][:])
             nc.scalar.activation(pairs[:, 0, :, j], rounded[:].indirect(offs_sb[:]), COPY)
         nc.vector.tensor_copy(pairs[:, 1, :, 0], planes[2][:].indirect(offs_sb[:]))
-        gate_sb = keep.tile([P, D, V], F32, name="gate_sb", tag="plane2", align_bytes=64)
+        gate_sb = keep.tile([P, D, V], F32, name="gate_sb", tag="rounded1", align_bytes=64)
         nc.scalar.dma_start(gate_sb[:], gate[:, 0:P, :].rearrange("d p v -> p d v"))
         quads = [keep.tile([P, QUARTER, 2, 2], BF16, name=f"quads{c}", align_bytes=64) for c in range(4)]
         pair_words = pairs[:].rearrange("p u n e -> p (u n e)").bitcast(F32).rearrange("p (u n) -> p u n", u=2)

@@ -63,34 +63,39 @@ def tile_picked_sub_lin_relu_sub_e_kernel(tc, xT, w_words, w_scales, b, gate, of
         nc.sync.dma_start(pos_sb[0][:], pos1)
         nc.sync.dma_start(pos_sb[1][:], pos2)
 
-        pairs = keep.tile([P, 2, S, 2], BF16, name="pairs", tag="pairs", align_bytes=64)
-        nc.vector.memset(pairs[:, 1, 3 * QUARTER :, :], 0.0)
+        pairs = keep.tile([P, 2, 3 * QUARTER, 2], BF16, name="pairs", tag="pairs", align_bytes=64)
+        late_pairs = keep.tile([P, 2, QUARTER, 2], BF16, name="late_pairs", align_bytes=64)
+        parts = ((pairs, 0, 3 * QUARTER), (late_pairs, 3 * QUARTER, S))
+        nc.vector.memset(pairs[:, 1, 2 * QUARTER :, :], 0.0)
         for j in range(2):
             rounded = keep.tile([P, T], BF16, name=f"rounded{j}", tag=f"rounded{j}", align_bytes=64)
             nc.vector.tensor_copy(rounded[:], planes[j][:])
-            nc.scalar.activation(pairs[:, 0, :, j], rounded[:].indirect(offs_sb[:]), COPY)
-        nc.vector.tensor_copy(pairs[:, 1, :, 0], planes[2][:].indirect(offs_sb[:]))
+            for target, lo, hi in parts:
+                nc.scalar.activation(target[:, 0, :, j], rounded[:].indirect(offs_sb[:, lo // 16 : hi // 16]), COPY)
+        for target, lo, hi in parts:
+            nc.vector.tensor_copy(target[:, 1, :, 0], planes[2][:].indirect(offs_sb[:, lo // 16 : hi // 16]))
         gate_sb = keep.tile([P, D, V], F32, name="gate_sb", tag="rounded1", align_bytes=64)
         nc.scalar.dma_start(gate_sb[:], gate[:, 0:P, :].rearrange("d p v -> p d v"))
         quads = [keep.tile([P, QUARTER, 2, 2], BF16, name=f"quads{c}", align_bytes=64) for c in range(4)]
-        pair_words = pairs[:].rearrange("p u n e -> p (u n e)").bitcast(F32).rearrange("p (u n) -> p u n", u=2)
 
-        def weave(c):
+        def weave(c, source, lo):
+            source_words = source[:].rearrange("p u n e -> p (u n e)").bitcast(F32).rearrange("p (u n) -> p u n", u=2)
             words = quads[c][:].rearrange("p n u e -> p (n u e)").bitcast(F32).rearrange("p (n u) -> p n u", u=2)
-            nc.scalar.copy(words, pair_words[:, :, c * QUARTER : (c + 1) * QUARTER].rearrange("p u n -> p n u"))
+            nc.scalar.copy(words, source_words[:, :, lo : lo + QUARTER].rearrange("p u n -> p n u"))
 
-        weave(3)
-        for c in range(3):
-            lo, hi = c * QUARTER, (c + 1) * QUARTER
-            nc.vector.tensor_copy(pairs[:, 1, lo:hi, 1], planes[3][:].indirect(offs_sb[:, lo // 16 : hi // 16]))
-            weave(c)
-        nc.vector.tensor_copy(quads[3][:, :, 1, 1], planes[3][:].indirect(offs_sb[:, 3 * QUARTER // 16 :]))
+        weave(2, pairs, 2 * QUARTER)
+        for c, source, lo in ((0, pairs, 0), (1, pairs, QUARTER), (3, late_pairs, 0)):
+            nc.vector.tensor_copy(
+                source[:, 1, lo : lo + QUARTER, 1], planes[3][:].indirect(offs_sb[:, c * QUARTER // 16 : (c + 1) * QUARTER // 16])
+            )
+            weave(c, source, lo)
+        nc.vector.tensor_copy(quads[2][:, :, 1, 1], planes[3][:].indirect(offs_sb[:, 2 * QUARTER // 16 : 3 * QUARTER // 16]))
 
-        x_codes = keep.tile([P, 3 * QUARTER], U32, name="x_codes", align_bytes=64)
-        last_codes = keep.tile([P, QUARTER], U32, name="last_codes", tag="pairs", align_bytes=64)
+        x_codes = keep.tile([P, 2 * QUARTER], U32, name="x_codes", align_bytes=64)
+        last_codes = keep.tile([P, 2 * QUARTER], U32, name="last_codes", tag="pairs", align_bytes=64)
 
         def codes(lo, hi):
-            return last_codes[:] if lo == 3 * QUARTER else x_codes[:, lo:hi]
+            return last_codes[:, lo - S // 2 : hi - S // 2] if lo >= S // 2 else x_codes[:, lo:hi]
 
         x_scale = keep.tile([P, S], U8, name="x_scale", align_bytes=64)
         y = [keep.tile([P, S], F32, name=f"y{h}", align_bytes=64) for h in range(HALVES)]
@@ -126,8 +131,7 @@ def tile_picked_sub_lin_relu_sub_e_kernel(tc, xT, w_words, w_scales, b, gate, of
         multiply(1, 0, 2 * QUARTER, front[:])
         rectify(1, 0, 2 * QUARTER, front[:])
         back = psum.tile([P, 2 * QUARTER], F32, name="back")
-        multiply(1, 2 * QUARTER, 3 * QUARTER, back[:, 0:QUARTER])
-        multiply(1, 3 * QUARTER, S, back[:, QUARTER:])
+        multiply(1, 2 * QUARTER, S, back[:])
         rectify(1, 2 * QUARTER, S, back[:])
 
         terms = keep.tile([P, D * HALVES, V], F32, name="terms", align_bytes=64)

@@ -31,9 +31,9 @@ def tile_picked_sub_lin_relu_sub_e_kernel(tc, xT, w_words, w_scales, b, gate, of
 
         offs_sb = keep.tile([P, S // 16], U16, name="offs_sb")
         pos_sb = [keep.tile([P, V // 16], U16, name=f"pos_sb{d}") for d in range(D)]
-        planes = [keep.tile([P, T], F32, name=f"plane{j}", tag=f"plane{j}", align_bytes=64) for j in range(PACK)]
-        w_codes = keep.tile([P, N], U32, name="w_codes", align_bytes=64)
-        w_scale = keep.tile([P, N], U8, name="w_scale", align_bytes=64)
+        planes = [keep.tile([P, T], F32, name=f"plane{j}", tag=f"plane{j}", align_bytes=256) for j in range(PACK)]
+        w_codes = keep.tile([P, N], U32, name="w_codes", align_bytes=256)
+        w_scale = keep.tile([P, N], U8, name="w_scale", align_bytes=256)
         bias = keep.tile([P, HALVES, 8], F32, name="bias")
         warm = keep.tile([P, 16], F32, name="warm")
 
@@ -63,20 +63,20 @@ def tile_picked_sub_lin_relu_sub_e_kernel(tc, xT, w_words, w_scales, b, gate, of
         nc.sync.dma_start(pos_sb[0][:], pos1)
         nc.sync.dma_start(pos_sb[1][:], pos2)
 
-        pairs = keep.tile([P, 2, 3 * QUARTER, 2], BF16, name="pairs", tag="pairs", align_bytes=64)
-        late_pairs = keep.tile([P, 2, QUARTER, 2], BF16, name="late_pairs", align_bytes=64)
+        pairs = keep.tile([P, 2, 3 * QUARTER, 2], BF16, name="pairs", tag="pairs", align_bytes=256)
+        late_pairs = keep.tile([P, 2, QUARTER, 2], BF16, name="late_pairs", align_bytes=256)
         parts = ((pairs, 0, 3 * QUARTER), (late_pairs, 3 * QUARTER, S))
         nc.vector.memset(pairs[:, 1, 2 * QUARTER :, :], 0.0)
         for j in range(2):
-            rounded = keep.tile([P, T], BF16, name=f"rounded{j}", tag=f"rounded{j}", align_bytes=64)
+            rounded = keep.tile([P, T], BF16, name=f"rounded{j}", tag=f"rounded{j}", align_bytes=256)
             nc.vector.tensor_copy(rounded[:], planes[j][:])
             for target, lo, hi in parts:
                 nc.scalar.activation(target[:, 0, :, j], rounded[:].indirect(offs_sb[:, lo // 16 : hi // 16]), COPY)
         for target, lo, hi in parts:
             nc.vector.tensor_copy(target[:, 1, :, 0], planes[2][:].indirect(offs_sb[:, lo // 16 : hi // 16]))
-        gate_sb = keep.tile([P, D, V], F32, name="gate_sb", tag="rounded1", align_bytes=64)
+        gate_sb = keep.tile([P, D, V], F32, name="gate_sb", tag="rounded1", align_bytes=256)
         nc.scalar.dma_start(gate_sb[:], gate[:, 0:P, :].rearrange("d p v -> p d v"))
-        quads = [keep.tile([P, QUARTER, 2, 2], BF16, name=f"quads{c}", align_bytes=64) for c in range(4)]
+        quads = [keep.tile([P, QUARTER, 2, 2], BF16, name=f"quads{c}", align_bytes=256) for c in range(4)]
 
         def weave(c, source, lo):
             source_words = source[:].rearrange("p u n e -> p (u n e)").bitcast(F32).rearrange("p (u n) -> p u n", u=2)
@@ -91,14 +91,14 @@ def tile_picked_sub_lin_relu_sub_e_kernel(tc, xT, w_words, w_scales, b, gate, of
             weave(c, source, lo)
         nc.vector.tensor_copy(quads[2][:, :, 1, 1], planes[3][:].indirect(offs_sb[:, 2 * QUARTER // 16 : 3 * QUARTER // 16]))
 
-        x_codes = keep.tile([P, 2 * QUARTER], U32, name="x_codes", align_bytes=64)
-        last_codes = keep.tile([P, 2 * QUARTER], U32, name="last_codes", tag="pairs", align_bytes=64)
+        x_codes = keep.tile([P, 2 * QUARTER], U32, name="x_codes", align_bytes=256)
+        last_codes = keep.tile([P, 2 * QUARTER], U32, name="last_codes", tag="pairs", align_bytes=256)
 
         def codes(lo, hi):
             return last_codes[:, lo - S // 2 : hi - S // 2] if lo >= S // 2 else x_codes[:, lo:hi]
 
-        x_scale = keep.tile([P, S], U8, name="x_scale", align_bytes=64)
-        y = [keep.tile([P, S], F32, name=f"y{h}", align_bytes=64) for h in range(HALVES)]
+        x_scale = keep.tile([P, S], U8, name="x_scale", align_bytes=256)
+        y = [keep.tile([P, S], F32, name=f"y{h}", align_bytes=256) for h in range(HALVES)]
 
         def quantise(lo, hi):
             nc.vector.quantize_mx(
@@ -134,8 +134,8 @@ def tile_picked_sub_lin_relu_sub_e_kernel(tc, xT, w_words, w_scales, b, gate, of
         multiply(1, 2 * QUARTER, S, back[:])
         rectify(1, 2 * QUARTER, S, back[:])
 
-        terms = keep.tile([P, D * HALVES, V], F32, name="terms", align_bytes=64)
-        total = [keep.tile([P, V], F32, name=f"total{h}", align_bytes=64) for h in range(HALVES)]
+        terms = keep.tile([P, D * HALVES, V], F32, name="terms", align_bytes=256)
+        total = [keep.tile([P, V], F32, name=f"total{h}", align_bytes=256) for h in range(HALVES)]
 
         def fetch(h, d):
             slot = d * HALVES + h

@@ -51,9 +51,9 @@ def tile_picked_sub_lin_relu_sub_e_kernel(tc, xT, w_words, w_scales, b, gate, of
                 w_scales[0, 4 * quadrant : 4 * quadrant + 4, :].bitcast(I32),
             )
 
-        load_plane(0)
+        load_plane(2)
         nc.sync.dma_start(offs_sb[:], offs)
-        for j in range(1, PACK):
+        for j in (0, 1, 3):
             load_plane(j)
         nc.sync.dma_start(w_codes[:].bitcast(I32), w_words[0].rearrange("p n r -> p (n r)").bitcast(I32))
         for quadrant in range(4):
@@ -67,14 +67,24 @@ def tile_picked_sub_lin_relu_sub_e_kernel(tc, xT, w_words, w_scales, b, gate, of
         late_pairs = keep.tile([P, 2, QUARTER, 2], BF16, name="late_pairs", align_bytes=256)
         parts = ((pairs, 0, 3 * QUARTER), (late_pairs, 3 * QUARTER, S))
         nc.vector.memset(pairs[:, 1, 2 * QUARTER :, :], 0.0)
-        for j in range(2):
+        def entries(lo, hi):
+            return offs_sb[:, lo // 16 : hi // 16]
+
+        def gather_pair_half(j, pieces, scalar_share):
             rounded = keep.tile([P, T], BF16, name=f"rounded{j}", tag=f"rounded{j}", align_bytes=256)
-            nc.vector.tensor_copy(rounded[:], planes[j][:])
-            for target, lo, hi in parts:
-                nc.scalar.activation(target[:, 0, :, j], rounded[:].indirect(offs_sb[:, lo // 16 : hi // 16]), COPY)
+            if scalar_share > 0:
+                nc.scalar.copy(rounded[:, 0:scalar_share], planes[j][:, 0:scalar_share])
+            if scalar_share < T:
+                nc.gpsimd.tensor_copy(rounded[:, scalar_share:], planes[j][:, scalar_share:])
+            for lo, hi in pieces:
+                nc.vector.tensor_copy(pairs[:, 0, lo:hi, j], planes[j][:].indirect(entries(lo, hi)))
+            nc.scalar.activation(late_pairs[:, 0, :, j], rounded[:].indirect(entries(3 * QUARTER, S)), COPY)
+
         for target, lo, hi in parts:
-            nc.vector.tensor_copy(target[:, 1, :, 0], planes[2][:].indirect(offs_sb[:, lo // 16 : hi // 16]))
-        gate_sb = keep.tile([P, D, V], F32, name="gate_sb", tag="rounded1", align_bytes=256)
+            nc.vector.tensor_copy(target[:, 1, :, 0], planes[2][:].indirect(entries(lo, hi)))
+        gather_pair_half(0, ((0, 3 * QUARTER),), 576)
+        gather_pair_half(1, ((2 * QUARTER, 3 * QUARTER), (0, 2 * QUARTER)), 320)
+        gate_sb = keep.tile([P, D, V], F32, name="gate_sb", tag="rounded0", align_bytes=256)
         nc.scalar.dma_start(gate_sb[:], gate[:, 0:P, :].rearrange("d p v -> p d v"))
         quads = [keep.tile([P, QUARTER, 2, 2], BF16, name=f"quads{c}", align_bytes=256) for c in range(4)]
 

@@ -82,8 +82,8 @@ def tile_picked_sub_lin_relu_sub_e_kernel(tc, xT, w_words, w_scales, b, gate, of
 
         for target, lo, hi in parts:
             nc.vector.tensor_copy(target[:, 1, :, 0], planes[2][:].indirect(entries(lo, hi)))
-        gather_pair_half(0, ((0, 3 * QUARTER),), 576)
-        gather_pair_half(1, ((2 * QUARTER, 3 * QUARTER), (0, 2 * QUARTER)), 320)
+        gather_pair_half(0, ((0, 3 * QUARTER),), 512)
+        gather_pair_half(1, ((2 * QUARTER, 3 * QUARTER), (0, 2 * QUARTER)), 256)
         gate_sb = keep.tile([P, D, V], F32, name="gate_sb", tag="rounded0", align_bytes=256)
         nc.scalar.dma_start(gate_sb[:], gate[:, 0:P, :].rearrange("d p v -> p d v"))
         quads = [keep.tile([P, QUARTER, 2, 2], BF16, name=f"quads{c}", align_bytes=256) for c in range(4)]

@@ -35,11 +35,8 @@ def tile_picked_sub_lin_relu_sub_e_kernel(tc, xT, w_words, w_scales, b, gate, of
         w_codes = keep.tile([P, N], U32, name="w_codes", align_bytes=256)
         w_scale = keep.tile([P, N], U8, name="w_scale", align_bytes=256)
         bias = keep.tile([P, HALVES, 8], F32, name="bias")
-        warm = keep.tile([P, 16], F32, name="warm")
 
-        nc.vector.memset(warm[:, 0:8], 0.0)
         nc.vector.memset(w_scale[:].bitcast(I32), 0)
-        nc.scalar.activation(warm[:, 8:16], warm[:, 0:8], RELU)
 
         x_rows = xT.rearrange("(p j) t -> p j t", j=PACK)
         def load_plane(j):

@@ -149,9 +149,9 @@ def tile_picked_sub_lin_relu_sub_e_kernel(tc, xT, w_words, w_scales, b, gate, of
             nc.vector.tensor_tensor(terms[:, slot, :], y[h][:].indirect(pos_sb[d][:]), gate_sb[:, d, :], MULT)
 
         def finish(h):
-            nc.vector.tensor_tensor(total[h][:], terms[:, h, :], terms[:, HALVES + h, :], ADD)
+            nc.vector.tensor_tensor(terms[:, h, :], terms[:, h, :], terms[:, HALVES + h, :], ADD)
             queue = nc.scalar if h == 0 else nc.sync
-            queue.dma_start(out[h * P : (h + 1) * P, :], total[h][:])
+            queue.dma_start(out[h * P : (h + 1) * P, :], terms[:, h, :])
 
         fetch(0, 0)
         fetch(0, 1)

@@ -52,9 +52,9 @@ def tile_picked_sub_lin_relu_sub_e_kernel(tc, xT, w_words, w_scales, b, gate, of
         nc.sync.dma_start(offs_sb[:], offs)
         for j in (0, 1, 3):
             load_plane(j)
-        nc.sync.dma_start(w_codes[:].bitcast(I32), w_words[0].rearrange("p n r -> p (n r)").bitcast(I32))
         for quadrant in range(4):
             load_scales(quadrant)
+        nc.sync.dma_start(w_codes[:].bitcast(I32), w_words[0].rearrange("p n r -> p (n r)").bitcast(I32))
         with nc.allow_non_contiguous_dma(reason="one bias value a partition"):
             nc.sync.dma_start(bias[:, :, 0:1], b.rearrange("(h p) o -> p h o", p=P))
         nc.sync.dma_start(pos_sb[0][:], pos1)
@@ -142,7 +142,6 @@ def tile_picked_sub_lin_relu_sub_e_kernel(tc, xT, w_words, w_scales, b, gate, of
         rectify(1, 2 * QUARTER, S, back[:])
 
         terms = keep.tile([P, D * HALVES, V], F32, name="terms", align_bytes=256)
-        total = [keep.tile([P, V], F32, name=f"total{h}", align_bytes=256) for h in range(HALVES)]
 
         def fetch(h, d):
             slot = d * HALVES + h

@@ -19,8 +19,10 @@ ADD = mybir.AluOpType.add
 
 P = 128
 PACK = 4
-HALVES = N // P
+ROW_TILES = N // P
 QUARTER = S // 4
+ALIGN = 256
+SCALAR_ROUNDS = (T // 2, T // 4)
 
 
 def tile_picked_sub_lin_relu_sub_e_kernel(tc, xT, w_words, w_scales, b, gate, offs, pos1, pos2, out):
@@ -31,92 +33,75 @@ def tile_picked_sub_lin_relu_sub_e_kernel(tc, xT, w_words, w_scales, b, gate, of
 
         offs_sb = keep.tile([P, S // 16], U16, name="offs_sb")
         pos_sb = [keep.tile([P, V // 16], U16, name=f"pos_sb{d}") for d in range(D)]
-        planes = [keep.tile([P, T], F32, name=f"plane{j}", tag=f"plane{j}", align_bytes=256) for j in range(PACK)]
-        w_codes = keep.tile([P, N], U32, name="w_codes", align_bytes=256)
-        w_scale = keep.tile([P, N], U8, name="w_scale", align_bytes=256)
-        bias = keep.tile([P, HALVES, 8], F32, name="bias")
+        planes = [keep.tile([P, T], F32, name=f"plane{j}", align_bytes=ALIGN) for j in range(PACK)]
+        w_codes = keep.tile([P, N], U32, name="w_codes", align_bytes=ALIGN)
+        w_scale = keep.tile([P, N], U8, name="w_scale", align_bytes=ALIGN)
+        bias = keep.tile([P, ROW_TILES, 8], F32, name="bias")
 
         nc.vector.memset(w_scale[:].bitcast(I32), 0)
 
         x_rows = xT.rearrange("(p j) t -> p j t", j=PACK)
-        def load_plane(j):
-            nc.sync.dma_start(planes[j][:], x_rows[:, j, :])
-
-        def load_scales(quadrant):
-            nc.sync.dma_start(
-                w_scale[32 * quadrant : 32 * quadrant + 4, :].bitcast(I32),
-                w_scales[0, 4 * quadrant : 4 * quadrant + 4, :].bitcast(I32),
-            )
-
-        load_plane(2)
+        nc.sync.dma_start(planes[2][:], x_rows[:, 2, :])
         nc.sync.dma_start(offs_sb[:], offs)
         for j in (0, 1, 3):
-            load_plane(j)
-        for quadrant in range(4):
-            load_scales(quadrant)
+            nc.sync.dma_start(planes[j][:], x_rows[:, j, :])
+        for q in range(4):
+            nc.sync.dma_start(w_scale[32 * q : 32 * q + 4, :].bitcast(I32), w_scales[0, 4 * q : 4 * q + 4, :].bitcast(I32))
         nc.sync.dma_start(w_codes[:].bitcast(I32), w_words[0].rearrange("p n r -> p (n r)").bitcast(I32))
         with nc.allow_non_contiguous_dma(reason="one bias value a partition"):
             nc.sync.dma_start(bias[:, :, 0:1], b.rearrange("(h p) o -> p h o", p=P))
         nc.sync.dma_start(pos_sb[0][:], pos1)
         nc.sync.dma_start(pos_sb[1][:], pos2)
 
-        pairs = keep.tile([P, 2, 3 * QUARTER, 2], BF16, name="pairs", tag="pairs", align_bytes=256)
-        late_pairs = keep.tile([P, 2, QUARTER, 2], BF16, name="late_pairs", align_bytes=256)
-        parts = ((pairs, 0, 3 * QUARTER), (late_pairs, 3 * QUARTER, S))
+        pairs = keep.tile([P, 2, 3 * QUARTER, 2], BF16, name="pairs", tag="pairs", align_bytes=ALIGN)
+        late_pairs = keep.tile([P, 2, QUARTER, 2], BF16, name="late_pairs", align_bytes=ALIGN)
         nc.vector.memset(pairs[:, 1, 2 * QUARTER :, :], 0.0)
+
         def entries(lo, hi):
             return offs_sb[:, lo // 16 : hi // 16]
 
-        def gather_pair_half(j, pieces, scalar_share):
-            rounded = keep.tile([P, T], BF16, name=f"rounded{j}", tag=f"rounded{j}", align_bytes=256)
-            if scalar_share > 0:
-                nc.scalar.copy(rounded[:, 0:scalar_share], planes[j][:, 0:scalar_share])
-            if scalar_share < T:
-                nc.gpsimd.tensor_copy(rounded[:, scalar_share:], planes[j][:, scalar_share:])
+        def gather_first_word(j, pieces):
+            share = SCALAR_ROUNDS[j]
+            rounded = keep.tile([P, T], BF16, name=f"rounded{j}", tag=f"rounded{j}", align_bytes=ALIGN)
+            nc.scalar.copy(rounded[:, 0:share], planes[j][:, 0:share])
+            nc.gpsimd.tensor_copy(rounded[:, share:], planes[j][:, share:])
             for lo, hi in pieces:
                 nc.vector.tensor_copy(pairs[:, 0, lo:hi, j], planes[j][:].indirect(entries(lo, hi)))
             nc.scalar.activation(late_pairs[:, 0, :, j], rounded[:].indirect(entries(3 * QUARTER, S)), COPY)
 
-        for target, lo, hi in parts:
-            nc.vector.tensor_copy(target[:, 1, :, 0], planes[2][:].indirect(entries(lo, hi)))
-        gather_pair_half(0, ((0, 3 * QUARTER),), 512)
-        gather_pair_half(1, ((2 * QUARTER, 3 * QUARTER), (0, 2 * QUARTER)), 256)
-        gate_sb = keep.tile([P, D, V], F32, name="gate_sb", tag="rounded0", align_bytes=256)
+        nc.vector.tensor_copy(pairs[:, 1, :, 0], planes[2][:].indirect(entries(0, 3 * QUARTER)))
+        nc.vector.tensor_copy(late_pairs[:, 1, :, 0], planes[2][:].indirect(entries(3 * QUARTER, S)))
+        gather_first_word(0, ((0, 3 * QUARTER),))
+        gather_first_word(1, ((2 * QUARTER, 3 * QUARTER), (0, 2 * QUARTER)))
+
+        gate_sb = keep.tile([P, D, V], F32, name="gate_sb", tag="rounded0", align_bytes=ALIGN)
         nc.scalar.dma_start(gate_sb[:], gate[:, 0:P, :].rearrange("d p v -> p d v"))
-        quads = [keep.tile([P, QUARTER, 2, 2], BF16, name=f"quads{c}", align_bytes=256) for c in range(4)]
+
+        quads = [keep.tile([P, QUARTER, 2, 2], BF16, name=f"quads{c}", align_bytes=ALIGN) for c in range(4)]
 
         def weave(c, source, lo):
             source_words = source[:].rearrange("p u n e -> p (u n e)").bitcast(F32).rearrange("p (u n) -> p u n", u=2)
-            words = quads[c][:].rearrange("p n u e -> p (n u e)").bitcast(F32).rearrange("p (n u) -> p n u", u=2)
-            nc.scalar.copy(words, source_words[:, :, lo : lo + QUARTER].rearrange("p u n -> p n u"))
+            quad_words = quads[c][:].rearrange("p n u e -> p (n u e)").bitcast(F32).rearrange("p (n u) -> p n u", u=2)
+            nc.scalar.copy(quad_words, source_words[:, :, lo : lo + QUARTER].rearrange("p u n -> p n u"))
 
         weave(2, pairs, 2 * QUARTER)
         for c, source, lo in ((0, pairs, 0), (1, pairs, QUARTER), (3, late_pairs, 0)):
-            nc.vector.tensor_copy(
-                source[:, 1, lo : lo + QUARTER, 1], planes[3][:].indirect(offs_sb[:, c * QUARTER // 16 : (c + 1) * QUARTER // 16])
-            )
+            nc.vector.tensor_copy(source[:, 1, lo : lo + QUARTER, 1], planes[3][:].indirect(entries(c * QUARTER, (c + 1) * QUARTER)))
             weave(c, source, lo)
-        nc.vector.tensor_copy(quads[2][:, :, 1, 1], planes[3][:].indirect(offs_sb[:, 2 * QUARTER // 16 : 3 * QUARTER // 16]))
+        nc.vector.tensor_copy(quads[2][:, :, 1, 1], planes[3][:].indirect(entries(2 * QUARTER, 3 * QUARTER)))
 
-        x_codes = keep.tile([P, 2 * QUARTER], U32, name="x_codes", align_bytes=256)
-        last_codes = keep.tile([P, 2 * QUARTER], U32, name="last_codes", tag="pairs", align_bytes=256)
+        front_codes = keep.tile([P, 2 * QUARTER], U32, name="front_codes", align_bytes=ALIGN)
+        back_codes = keep.tile([P, 2 * QUARTER], U32, name="back_codes", tag="pairs", align_bytes=ALIGN)
+        x_scale = keep.tile([P, S], U8, name="x_scale", align_bytes=ALIGN)
+        y = [keep.tile([P, S], F32, name=f"y{h}", align_bytes=ALIGN) for h in range(ROW_TILES)]
 
         def codes(lo, hi):
-            return last_codes[:, lo - S // 2 : hi - S // 2] if lo >= S // 2 else x_codes[:, lo:hi]
+            return back_codes[:, lo - S // 2 : hi - S // 2] if lo >= S // 2 else front_codes[:, lo:hi]
 
-        x_scale = keep.tile([P, S], U8, name="x_scale", align_bytes=256)
-        y = [keep.tile([P, S], F32, name=f"y{h}", align_bytes=256) for h in range(HALVES)]
-
-        def quantise(lo, hi):
-            nc.vector.quantize_mx(
-                out=codes(lo, hi).bitcast(FP8X4),
-                scales=x_scale[:, lo:hi],
-                in_=quads[lo // QUARTER][:].rearrange("p n u e -> p (n u e)"),
-            )
-
-        def multiply(h, lo, hi, target):
+        def layer(h, lo, hi, bank_name):
+            bank = psum.tile([P, hi - lo], F32, name=bank_name)
             nc.tensor.matmul_mx(
-                out=target,
+                out=bank[:],
                 lhsT=w_codes[:, h * P : (h + 1) * P].bitcast(FP8X4),
                 lhsT_scale=w_scale[:, h * P : (h + 1) * P],
                 rhs=codes(lo, hi).bitcast(FP8X4),
@@ -124,37 +109,21 @@ def tile_picked_sub_lin_relu_sub_e_kernel(tc, xT, w_words, w_scales, b, gate, of
                 start=True,
                 stop=True,
             )
-
-        def rectify(h, lo, hi, bank):
-            nc.scalar.activation(y[h][:, lo:hi], bank, RELU, bias=bias[:, h, 0:1])
+            nc.scalar.activation(y[h][:, lo:hi], bank[:], RELU, bias=bias[:, h, 0:1])
 
         for c in range(4):
             lo, hi = c * QUARTER, (c + 1) * QUARTER
-            bank = psum.tile([P, QUARTER], F32, name=f"first{c}")
-            quantise(lo, hi)
-            multiply(0, lo, hi, bank[:])
-            rectify(0, lo, hi, bank[:])
-        front = psum.tile([P, 2 * QUARTER], F32, name="front")
-        multiply(1, 0, 2 * QUARTER, front[:])
-        rectify(1, 0, 2 * QUARTER, front[:])
-        back = psum.tile([P, 2 * QUARTER], F32, name="back")
-        multiply(1, 2 * QUARTER, S, back[:])
-        rectify(1, 2 * QUARTER, S, back[:])
+            nc.vector.quantize_mx(
+                out=codes(lo, hi).bitcast(FP8X4), scales=x_scale[:, lo:hi], in_=quads[c][:].rearrange("p n u e -> p (n u e)")
+            )
+            layer(0, lo, hi, f"first{c}")
+        layer(1, 0, S // 2, "front")
+        layer(1, S // 2, S, "back")
 
-        terms = keep.tile([P, D * HALVES, V], F32, name="terms", align_bytes=256)
-
-        def fetch(h, d):
-            slot = d * HALVES + h
-            nc.vector.tensor_tensor(terms[:, slot, :], y[h][:].indirect(pos_sb[d][:]), gate_sb[:, d, :], MULT)
-
-        def finish(h):
-            nc.vector.tensor_tensor(terms[:, h, :], terms[:, h, :], terms[:, HALVES + h, :], ADD)
-            queue = nc.scalar if h == 0 else nc.sync
-            queue.dma_start(out[h * P : (h + 1) * P, :], terms[:, h, :])
-
-        fetch(0, 0)
-        fetch(0, 1)
-        fetch(1, 0)
-        fetch(1, 1)
-        finish(0)
-        finish(1)
+        terms = keep.tile([P, D, ROW_TILES, V], F32, name="terms", align_bytes=ALIGN)
+        for h in range(ROW_TILES):
+            for d in range(D):
+                nc.vector.tensor_tensor(terms[:, d, h, :], y[h][:].indirect(pos_sb[d][:]), gate_sb[:, d, :], MULT)
+        for h, queue in enumerate((nc.scalar, nc.sync)):
+            nc.vector.tensor_tensor(terms[:, 0, h, :], terms[:, 0, h, :], terms[:, 1, h, :], ADD)
+            queue.dma_start(out[h * P : (h + 1) * P, :], terms[:, 0, h, :])

@@ -117,8 +117,8 @@ def tile_picked_sub_lin_relu_sub_e_kernel(tc, xT, w_words, w_scales, b, gate, of
                 out=codes(lo, hi).bitcast(FP8X4), scales=x_scale[:, lo:hi], in_=quads[c][:].rearrange("p n u e -> p (n u e)")
             )
             layer(0, lo, hi, f"first{c}")
-        layer(1, 0, S // 2, "front")
-        layer(1, S // 2, S, "back")
+        for c in range(4):
+            layer(1, c * QUARTER, (c + 1) * QUARTER, f"second{c}")
 
         terms = keep.tile([P, D, ROW_TILES, V], F32, name="terms", align_bytes=ALIGN)
         for h in range(ROW_TILES):

@@ -77,18 +77,19 @@ def tile_picked_sub_lin_relu_sub_e_kernel(tc, xT, w_words, w_scales, b, gate, of
         gate_sb = keep.tile([P, D, V], F32, name="gate_sb", tag="rounded0", align_bytes=ALIGN)
         nc.scalar.dma_start(gate_sb[:], gate[:, 0:P, :].rearrange("d p v -> p d v"))
 
-        quads = [keep.tile([P, QUARTER, 2, 2], BF16, name=f"quads{c}", align_bytes=ALIGN) for c in range(4)]
+        all_quads = keep.tile([P, 4, QUARTER, 2, 2], BF16, name="all_quads", align_bytes=ALIGN)
+        quads = [all_quads[:, c, :, :, :] for c in range(4)]
 
         def weave(c, source, lo):
             source_words = source[:].rearrange("p u n e -> p (u n e)").bitcast(F32).rearrange("p (u n) -> p u n", u=2)
-            quad_words = quads[c][:].rearrange("p n u e -> p (n u e)").bitcast(F32).rearrange("p (n u) -> p n u", u=2)
+            quad_words = quads[c].rearrange("p n u e -> p (n u e)").bitcast(F32).rearrange("p (n u) -> p n u", u=2)
             nc.scalar.copy(quad_words, source_words[:, :, lo : lo + QUARTER].rearrange("p u n -> p n u"))
 
         weave(2, pairs, 2 * QUARTER)
         for c, source, lo in ((0, pairs, 0), (1, pairs, QUARTER), (3, late_pairs, 0)):
             nc.vector.tensor_copy(source[:, 1, lo : lo + QUARTER, 1], planes[3][:].indirect(entries(c * QUARTER, (c + 1) * QUARTER)))
             weave(c, source, lo)
-        nc.vector.tensor_copy(quads[2][:, :, 1, 1], planes[3][:].indirect(entries(2 * QUARTER, 3 * QUARTER)))
+        nc.vector.tensor_copy(all_quads[:, 2, :, 1, 1], planes[3][:].indirect(entries(2 * QUARTER, 3 * QUARTER)))
 
         front_codes = keep.tile([P, 2 * QUARTER], U32, name="front_codes", align_bytes=ALIGN)
         back_codes = keep.tile([P, 2 * QUARTER], U32, name="back_codes", tag="pairs", align_bytes=ALIGN)
@@ -114,7 +115,7 @@ def tile_picked_sub_lin_relu_sub_e_kernel(tc, xT, w_words, w_scales, b, gate, of
         for c in range(4):
             lo, hi = c * QUARTER, (c + 1) * QUARTER
             nc.vector.quantize_mx(
-                out=codes(lo, hi).bitcast(FP8X4), scales=x_scale[:, lo:hi], in_=quads[c][:].rearrange("p n u e -> p (n u e)")
+                out=codes(lo, hi).bitcast(FP8X4), scales=x_scale[:, lo:hi], in_=quads[c].rearrange("p n u e -> p (n u e)")
             )
             layer(0, lo, hi, f"first{c}")
         for c in range(4):

@@ -60,36 +60,34 @@ def tile_picked_sub_lin_relu_sub_e_kernel(tc, xT, w_words, w_scales, b, gate, of
         def entries(lo, hi):
             return offs_sb[:, lo // 16 : hi // 16]
 
-        def gather_first_word(j, pieces):
+        def gather_first_word(j):
             share = SCALAR_ROUNDS[j]
             rounded = keep.tile([P, T], BF16, name=f"rounded{j}", tag=f"rounded{j}", align_bytes=ALIGN)
             nc.scalar.copy(rounded[:, 0:share], planes[j][:, 0:share])
             nc.gpsimd.tensor_copy(rounded[:, share:], planes[j][:, share:])
-            for lo, hi in pieces:
-                nc.vector.tensor_copy(pairs[:, 0, lo:hi, j], planes[j][:].indirect(entries(lo, hi)))
+            nc.vector.tensor_copy(pairs[:, 0, :, j], planes[j][:].indirect(entries(0, 3 * QUARTER)))
             nc.scalar.activation(late_pairs[:, 0, :, j], rounded[:].indirect(entries(3 * QUARTER, S)), COPY)
 
         nc.vector.tensor_copy(pairs[:, 1, :, 0], planes[2][:].indirect(entries(0, 3 * QUARTER)))
         nc.vector.tensor_copy(late_pairs[:, 1, :, 0], planes[2][:].indirect(entries(3 * QUARTER, S)))
-        gather_first_word(0, ((0, 3 * QUARTER),))
-        gather_first_word(1, ((2 * QUARTER, 3 * QUARTER), (0, 2 * QUARTER)))
+        gather_first_word(0)
+        gather_first_word(1)
 
         gate_sb = keep.tile([P, D, V], F32, name="gate_sb", tag="rounded0", align_bytes=ALIGN)
         nc.scalar.dma_start(gate_sb[:], gate[:, 0:P, :].rearrange("d p v -> p d v"))
 
-        all_quads = keep.tile([P, 4, QUARTER, 2, 2], BF16, name="all_quads", align_bytes=ALIGN)
-        quads = [all_quads[:, c, :, :, :] for c in range(4)]
+        quads = keep.tile([P, 4, QUARTER, 2, 2], BF16, name="quads", align_bytes=ALIGN)
 
         def weave(c, source, lo):
             source_words = source[:].rearrange("p u n e -> p (u n e)").bitcast(F32).rearrange("p (u n) -> p u n", u=2)
-            quad_words = quads[c].rearrange("p n u e -> p (n u e)").bitcast(F32).rearrange("p (n u) -> p n u", u=2)
+            quad_words = quads[:, c, :, :, :].rearrange("p n u e -> p (n u e)").bitcast(F32).rearrange("p (n u) -> p n u", u=2)
             nc.scalar.copy(quad_words, source_words[:, :, lo : lo + QUARTER].rearrange("p u n -> p n u"))
 
         weave(2, pairs, 2 * QUARTER)
         for c, source, lo in ((0, pairs, 0), (1, pairs, QUARTER), (3, late_pairs, 0)):
             nc.vector.tensor_copy(source[:, 1, lo : lo + QUARTER, 1], planes[3][:].indirect(entries(c * QUARTER, (c + 1) * QUARTER)))
             weave(c, source, lo)
-        nc.vector.tensor_copy(all_quads[:, 2, :, 1, 1], planes[3][:].indirect(entries(2 * QUARTER, 3 * QUARTER)))
+        nc.vector.tensor_copy(quads[:, 2, :, 1, 1], planes[3][:].indirect(entries(2 * QUARTER, 3 * QUARTER)))
 
         front_codes = keep.tile([P, 2 * QUARTER], U32, name="front_codes", align_bytes=ALIGN)
         back_codes = keep.tile([P, 2 * QUARTER], U32, name="back_codes", tag="pairs", align_bytes=ALIGN)
@@ -115,7 +113,7 @@ def tile_picked_sub_lin_relu_sub_e_kernel(tc, xT, w_words, w_scales, b, gate, of
         for c in range(4):
             lo, hi = c * QUARTER, (c + 1) * QUARTER
             nc.vector.quantize_mx(
-                out=codes(lo, hi).bitcast(FP8X4), scales=x_scale[:, lo:hi], in_=quads[c].rearrange("p n u e -> p (n u e)")
+                out=codes(lo, hi).bitcast(FP8X4), scales=x_scale[:, lo:hi], in_=quads[:, c, :, :, :].rearrange("p n u e -> p (n u e)")
             )
             layer(0, lo, hi, f"first{c}")
         for c in range(4):

@@ -22,7 +22,7 @@ PACK = 4
 ROW_TILES = N // P
 QUARTER = S // 4
 ALIGN = 256
-SCALAR_ROUNDS = (T // 2, T // 4)
+SCALAR_ROUNDS = (T // 2, T // 2)
 
 
 def tile_picked_sub_lin_relu_sub_e_kernel(tc, xT, w_words, w_scales, b, gate, offs, pos1, pos2, out):

@@ -22,7 +22,7 @@ PACK = 4
 ROW_TILES = N // P
 QUARTER = S // 4
 ALIGN = 256
-SCALAR_ROUNDS = (T // 2, T // 2)
+SCALAR_ROUNDS = T // 2
 
 
 def tile_picked_sub_lin_relu_sub_e_kernel(tc, xT, w_words, w_scales, b, gate, offs, pos1, pos2, out):
@@ -45,8 +45,11 @@ def tile_picked_sub_lin_relu_sub_e_kernel(tc, xT, w_words, w_scales, b, gate, of
         nc.sync.dma_start(offs_sb[:], offs)
         for j in (0, 1, 3):
             nc.sync.dma_start(planes[j][:], x_rows[:, j, :])
-        for q in range(4):
-            nc.sync.dma_start(w_scale[32 * q : 32 * q + 4, :].bitcast(I32), w_scales[0, 4 * q : 4 * q + 4, :].bitcast(I32))
+        for quadrant in range(4):
+            nc.sync.dma_start(
+                w_scale[32 * quadrant : 32 * quadrant + 4, :].bitcast(I32),
+                w_scales[0, 4 * quadrant : 4 * quadrant + 4, :].bitcast(I32),
+            )
         nc.sync.dma_start(w_codes[:].bitcast(I32), w_words[0].rearrange("p n r -> p (n r)").bitcast(I32))
         with nc.allow_non_contiguous_dma(reason="one bias value a partition"):
             nc.sync.dma_start(bias[:, :, 0:1], b.rearrange("(h p) o -> p h o", p=P))
@@ -61,10 +64,9 @@ def tile_picked_sub_lin_relu_sub_e_kernel(tc, xT, w_words, w_scales, b, gate, of
             return offs_sb[:, lo // 16 : hi // 16]
 
         def gather_first_word(j):
-            share = SCALAR_ROUNDS[j]
             rounded = keep.tile([P, T], BF16, name=f"rounded{j}", tag=f"rounded{j}", align_bytes=ALIGN)
-            nc.scalar.copy(rounded[:, 0:share], planes[j][:, 0:share])
-            nc.gpsimd.tensor_copy(rounded[:, share:], planes[j][:, share:])
+            nc.scalar.copy(rounded[:, 0:SCALAR_ROUNDS], planes[j][:, 0:SCALAR_ROUNDS])
+            nc.gpsimd.tensor_copy(rounded[:, SCALAR_ROUNDS:], planes[j][:, SCALAR_ROUNDS:])
             nc.vector.tensor_copy(pairs[:, 0, :, j], planes[j][:].indirect(entries(0, 3 * QUARTER)))
             nc.scalar.activation(late_pairs[:, 0, :, j], rounded[:].indirect(entries(3 * QUARTER, S)), COPY)
 
@@ -94,30 +96,32 @@ def tile_picked_sub_lin_relu_sub_e_kernel(tc, xT, w_words, w_scales, b, gate, of
         x_scale = keep.tile([P, S], U8, name="x_scale", align_bytes=ALIGN)
         y = [keep.tile([P, S], F32, name=f"y{h}", align_bytes=ALIGN) for h in range(ROW_TILES)]
 
-        def codes(lo, hi):
-            return back_codes[:, lo - S // 2 : hi - S // 2] if lo >= S // 2 else front_codes[:, lo:hi]
+        def codes(c):
+            return (front_codes, back_codes)[c // 2][:, c % 2 * QUARTER : (c % 2 + 1) * QUARTER].bitcast(FP8X4)
 
-        def layer(h, lo, hi, bank_name):
-            bank = psum.tile([P, hi - lo], F32, name=bank_name)
+        def layer(h, c):
+            columns = slice(c * QUARTER, (c + 1) * QUARTER)
+            bank = psum.tile([P, QUARTER], F32, name=f"bank{h}{c}")
             nc.tensor.matmul_mx(
                 out=bank[:],
                 lhsT=w_codes[:, h * P : (h + 1) * P].bitcast(FP8X4),
                 lhsT_scale=w_scale[:, h * P : (h + 1) * P],
-                rhs=codes(lo, hi).bitcast(FP8X4),
-                rhs_scale=x_scale[:, lo:hi],
+                rhs=codes(c),
+                rhs_scale=x_scale[:, columns],
                 start=True,
                 stop=True,
             )
-            nc.scalar.activation(y[h][:, lo:hi], bank[:], RELU, bias=bias[:, h, 0:1])
+            nc.scalar.activation(y[h][:, columns], bank[:], RELU, bias=bias[:, h, 0:1])
 
         for c in range(4):
-            lo, hi = c * QUARTER, (c + 1) * QUARTER
             nc.vector.quantize_mx(
-                out=codes(lo, hi).bitcast(FP8X4), scales=x_scale[:, lo:hi], in_=quads[:, c, :, :, :].rearrange("p n u e -> p (n u e)")
+                out=codes(c),
+                scales=x_scale[:, c * QUARTER : (c + 1) * QUARTER],
+                in_=quads[:, c, :, :, :].rearrange("p n u e -> p (n u e)"),
             )
-            layer(0, lo, hi, f"first{c}")
+            layer(0, c)
         for c in range(4):
-            layer(1, c * QUARTER, (c + 1) * QUARTER, f"second{c}")
+            layer(1, c)
 
         terms = keep.tile([P, D, ROW_TILES, V], F32, name="terms", align_bytes=ALIGN)
         for h in range(ROW_TILES):

@@ -36,7 +36,7 @@ def tile_picked_sub_lin_relu_sub_e_kernel(tc, xT, w_words, w_scales, b, gate, of
         planes = [keep.tile([P, T], F32, name=f"plane{j}", align_bytes=ALIGN) for j in range(PACK)]
         w_codes = keep.tile([P, N], U32, name="w_codes", align_bytes=ALIGN)
         w_scale = keep.tile([P, N], U8, name="w_scale", align_bytes=ALIGN)
-        bias = keep.tile([P, ROW_TILES, 8], F32, name="bias")
+        bias = keep.tile([P, ROW_TILES, 1], F32, name="bias")
 
         nc.vector.memset(w_scale[:].bitcast(I32), 0)
 

@@ -52,7 +52,7 @@ def tile_picked_sub_lin_relu_sub_e_kernel(tc, xT, w_words, w_scales, b, gate, of
             )
         nc.sync.dma_start(w_codes[:].bitcast(I32), w_words[0].rearrange("p n r -> p (n r)").bitcast(I32))
         with nc.allow_non_contiguous_dma(reason="one bias value a partition"):
-            nc.sync.dma_start(bias[:, :, 0:1], b.rearrange("(h p) o -> p h o", p=P))
+            nc.sync.dma_start(bias[:], b.rearrange("(h p) o -> p h o", p=P))
         nc.sync.dma_start(pos_sb[0][:], pos1)
         nc.sync.dma_start(pos_sb[1][:], pos2)
 
@@ -111,7 +111,7 @@ def tile_picked_sub_lin_relu_sub_e_kernel(tc, xT, w_words, w_scales, b, gate, of
                 start=True,
                 stop=True,
             )
-            nc.scalar.activation(y[h][:, columns], bank[:], RELU, bias=bias[:, h, 0:1])
+            nc.scalar.activation(y[h][:, columns], bank[:], RELU, bias=bias[:, h, :])
 
         for c in range(4):
             nc.vector.quantize_mx(

@@ -57,7 +57,7 @@ def tile_picked_sub_lin_relu_sub_e_kernel(tc, xT, w_words, w_scales, b, gate, of
         nc.sync.dma_start(pos_sb[1][:], pos2)
 
         pairs = keep.tile([P, 2, 3 * QUARTER, 2], BF16, name="pairs", tag="pairs", align_bytes=ALIGN)
-        late_pairs = keep.tile([P, 2, QUARTER, 2], BF16, name="late_pairs", align_bytes=ALIGN)
+        late_pairs = keep.tile([P, 2, QUARTER, 2], BF16, name="late_pairs", tag="late_pairs", align_bytes=ALIGN)
         nc.vector.memset(pairs[:, 1, 2 * QUARTER :, :], 0.0)
 
         def entries(lo, hi):
@@ -78,18 +78,20 @@ def tile_picked_sub_lin_relu_sub_e_kernel(tc, xT, w_words, w_scales, b, gate, of
         gate_sb = keep.tile([P, D, V], F32, name="gate_sb", tag="rounded0", align_bytes=ALIGN)
         nc.scalar.dma_start(gate_sb[:], gate[:, 0:P, :].rearrange("d p v -> p d v"))
 
-        quads = keep.tile([P, 4, QUARTER, 2, 2], BF16, name="quads", align_bytes=ALIGN)
+        quads = [keep.tile([P, QUARTER, 2, 2], BF16, name=f"quads{c}", align_bytes=ALIGN) for c in range(4)]
 
-        def weave(c, source, lo):
-            source_words = source[:].rearrange("p u n e -> p (u n e)").bitcast(F32).rearrange("p (u n) -> p u n", u=2)
-            quad_words = quads[:, c, :, :, :].rearrange("p n u e -> p (n u e)").bitcast(F32).rearrange("p (n u) -> p n u", u=2)
-            nc.scalar.copy(quad_words, source_words[:, :, lo : lo + QUARTER].rearrange("p u n -> p n u"))
+        def weave(c, source, lo, copy=nc.scalar.copy, word=F32):
+            source_words = source[:].rearrange("p u n e -> p (u n e)").bitcast(word).rearrange("p (u n) -> p u n", u=2)
+            quad_words = quads[c][:].rearrange("p n u e -> p (n u e)").bitcast(word).rearrange("p (n u) -> p n u", u=2)
+            copy(quad_words, source_words[:, :, lo : lo + QUARTER].rearrange("p u n -> p n u"))
 
         weave(2, pairs, 2 * QUARTER)
-        for c, source, lo in ((0, pairs, 0), (1, pairs, QUARTER), (3, late_pairs, 0)):
-            nc.vector.tensor_copy(source[:, 1, lo : lo + QUARTER, 1], planes[3][:].indirect(entries(c * QUARTER, (c + 1) * QUARTER)))
-            weave(c, source, lo)
-        nc.vector.tensor_copy(quads[:, 2, :, 1, 1], planes[3][:].indirect(entries(2 * QUARTER, 3 * QUARTER)))
+        nc.vector.tensor_copy(pairs[:, 1, 0 : 2 * QUARTER, 1], planes[3][:].indirect(entries(0, 2 * QUARTER)))
+        weave(0, pairs, 0)
+        weave(1, pairs, QUARTER, nc.gpsimd.tensor_copy, U32)
+        nc.vector.tensor_copy(late_pairs[:, 1, :, 1], planes[3][:].indirect(entries(3 * QUARTER, S)))
+        weave(3, late_pairs, 0)
+        nc.vector.tensor_copy(quads[2][:, :, 1, 1], planes[3][:].indirect(entries(2 * QUARTER, 3 * QUARTER)))
 
         front_codes = keep.tile([P, 2 * QUARTER], U32, name="front_codes", align_bytes=ALIGN)
         back_codes = keep.tile([P, 2 * QUARTER], U32, name="back_codes", tag="pairs", align_bytes=ALIGN)
@@ -97,7 +99,7 @@ def tile_picked_sub_lin_relu_sub_e_kernel(tc, xT, w_words, w_scales, b, gate, of
         y = [keep.tile([P, S], F32, name=f"y{h}", align_bytes=ALIGN) for h in range(ROW_TILES)]
 
         def codes(c):
-            return (front_codes, back_codes)[c // 2][:, c % 2 * QUARTER : (c % 2 + 1) * QUARTER].bitcast(FP8X4)
+            return (front_codes, back_codes, back_codes, front_codes)[c][:, c % 2 * QUARTER : (c % 2 + 1) * QUARTER].bitcast(FP8X4)
 
         def layer(h, c):
             columns = slice(c * QUARTER, (c + 1) * QUARTER)
@@ -117,7 +119,7 @@ def tile_picked_sub_lin_relu_sub_e_kernel(tc, xT, w_words, w_scales, b, gate, of
             nc.vector.quantize_mx(
                 out=codes(c),
                 scales=x_scale[:, c * QUARTER : (c + 1) * QUARTER],
-                in_=quads[:, c, :, :, :].rearrange("p n u e -> p (n u e)"),
+                in_=quads[c][:].rearrange("p n u e -> p (n u e)"),
             )
             layer(0, c)
         for c in range(4):

@@ -22,6 +22,7 @@ PACK = 4
 ROW_TILES = N // P
 QUARTER = S // 4
 ALIGN = 256
+GPSIMD_WEAVES = 80
 SCALAR_ROUNDS = T // 2
 
 
@@ -78,20 +79,21 @@ def tile_picked_sub_lin_relu_sub_e_kernel(tc, xT, w_words, w_scales, b, gate, of
         gate_sb = keep.tile([P, D, V], F32, name="gate_sb", tag="rounded0", align_bytes=ALIGN)
         nc.scalar.dma_start(gate_sb[:], gate[:, 0:P, :].rearrange("d p v -> p d v"))
 
-        quads = [keep.tile([P, QUARTER, 2, 2], BF16, name=f"quads{c}", align_bytes=ALIGN) for c in range(4)]
+        quads = keep.tile([P, S, 2, 2], BF16, name="quads", align_bytes=ALIGN)
 
-        def weave(c, source, lo, copy=nc.scalar.copy, word=F32):
-            source_words = source[:].rearrange("p u n e -> p (u n e)").bitcast(word).rearrange("p (u n) -> p u n", u=2)
-            quad_words = quads[c][:].rearrange("p n u e -> p (n u e)").bitcast(word).rearrange("p (n u) -> p n u", u=2)
-            copy(quad_words, source_words[:, :, lo : lo + QUARTER].rearrange("p u n -> p n u"))
+        def weave(source, first, lo, hi, copy=nc.scalar.copy, word=F32):
+            source_words = source[:].rearrange("p u n e -> p (u n e)").bitcast(word).rearrange("p (u n) -> p n u", u=2)
+            quad_words = quads[:, lo:hi, :, :].rearrange("p n u e -> p (n u e)").bitcast(word).rearrange("p (n u) -> p n u", u=2)
+            copy(quad_words, source_words[:, lo - first : hi - first, :])
 
-        weave(2, pairs, 2 * QUARTER)
+        weave(pairs, 0, 2 * QUARTER, 3 * QUARTER)
         nc.vector.tensor_copy(pairs[:, 1, 0 : 2 * QUARTER, 1], planes[3][:].indirect(entries(0, 2 * QUARTER)))
-        weave(0, pairs, 0)
-        weave(1, pairs, QUARTER, nc.gpsimd.tensor_copy, U32)
+        weave(pairs, 0, 0, GPSIMD_WEAVES, nc.gpsimd.tensor_copy, U32)
+        weave(pairs, 0, GPSIMD_WEAVES, QUARTER)
+        weave(pairs, 0, QUARTER, 2 * QUARTER)
         nc.vector.tensor_copy(late_pairs[:, 1, :, 1], planes[3][:].indirect(entries(3 * QUARTER, S)))
-        weave(3, late_pairs, 0)
-        nc.vector.tensor_copy(quads[2][:, :, 1, 1], planes[3][:].indirect(entries(2 * QUARTER, 3 * QUARTER)))
+        weave(late_pairs, 3 * QUARTER, 3 * QUARTER, S)
+        nc.vector.tensor_copy(quads[:, 2 * QUARTER : 3 * QUARTER, 1, 1], planes[3][:].indirect(entries(2 * QUARTER, 3 * QUARTER)))
 
         front_codes = keep.tile([P, 2 * QUARTER], U32, name="front_codes", align_bytes=ALIGN)
         back_codes = keep.tile([P, 2 * QUARTER], U32, name="back_codes", tag="pairs", align_bytes=ALIGN)
@@ -99,7 +101,7 @@ def tile_picked_sub_lin_relu_sub_e_kernel(tc, xT, w_words, w_scales, b, gate, of
         y = [keep.tile([P, S], F32, name=f"y{h}", align_bytes=ALIGN) for h in range(ROW_TILES)]
 
         def codes(c):
-            return (front_codes, back_codes, back_codes, front_codes)[c][:, c % 2 * QUARTER : (c % 2 + 1) * QUARTER].bitcast(FP8X4)
+            return (front_codes, back_codes)[c // 2][:, c % 2 * QUARTER : (c % 2 + 1) * QUARTER].bitcast(FP8X4)
 
         def layer(h, c):
             columns = slice(c * QUARTER, (c + 1) * QUARTER)
@@ -119,7 +121,7 @@ def tile_picked_sub_lin_relu_sub_e_kernel(tc, xT, w_words, w_scales, b, gate, of
             nc.vector.quantize_mx(
                 out=codes(c),
                 scales=x_scale[:, c * QUARTER : (c + 1) * QUARTER],
-                in_=quads[c][:].rearrange("p n u e -> p (n u e)"),
+                in_=quads[:, c * QUARTER : (c + 1) * QUARTER, :, :].rearrange("p n u e -> p (n u e)"),
             )
             layer(0, c)
         for c in range(4):

@@ -21,9 +21,8 @@ P = 128
 PACK = 4
 ROW_TILES = N // P
 QUARTER = S // 4
+HALF = S // 2
 ALIGN = 256
-GPSIMD_WEAVES = 80
-SCALAR_ROUNDS = T // 2
 
 
 def tile_picked_sub_lin_relu_sub_e_kernel(tc, xT, w_words, w_scales, b, gate, offs, pos1, pos2, out):
@@ -38,13 +37,17 @@ def tile_picked_sub_lin_relu_sub_e_kernel(tc, xT, w_words, w_scales, b, gate, of
         w_codes = keep.tile([P, N], U32, name="w_codes", align_bytes=ALIGN)
         w_scale = keep.tile([P, N], U8, name="w_scale", align_bytes=ALIGN)
         bias = keep.tile([P, ROW_TILES, 1], F32, name="bias")
+        gate_sb = keep.tile([P, D, V], F32, name="gate_sb", align_bytes=ALIGN)
 
         nc.vector.memset(w_scale[:].bitcast(I32), 0)
+        warm = keep.tile([P, 2], F32, name="warm")
+        nc.vector.memset(warm[:, 0:1], 0.0)
+        nc.scalar.copy(warm[:, 1:2], warm[:, 0:1])
 
         x_rows = xT.rearrange("(p j) t -> p j t", j=PACK)
-        nc.sync.dma_start(planes[2][:], x_rows[:, 2, :])
+        nc.sync.dma_start(planes[0][:], x_rows[:, 0, :])
         nc.sync.dma_start(offs_sb[:], offs)
-        for j in (0, 1, 3):
+        for j in (1, 2, 3):
             nc.sync.dma_start(planes[j][:], x_rows[:, j, :])
         for quadrant in range(4):
             nc.sync.dma_start(
@@ -54,54 +57,48 @@ def tile_picked_sub_lin_relu_sub_e_kernel(tc, xT, w_words, w_scales, b, gate, of
         nc.sync.dma_start(w_codes[:].bitcast(I32), w_words[0].rearrange("p n r -> p (n r)").bitcast(I32))
         with nc.allow_non_contiguous_dma(reason="one bias value a partition"):
             nc.sync.dma_start(bias[:], b.rearrange("(h p) o -> p h o", p=P))
+        nc.sync.dma_start(gate_sb[:], gate[:, 0:P, :].rearrange("d p v -> p d v"))
         nc.sync.dma_start(pos_sb[0][:], pos1)
         nc.sync.dma_start(pos_sb[1][:], pos2)
-
-        pairs = keep.tile([P, 2, 3 * QUARTER, 2], BF16, name="pairs", tag="pairs", align_bytes=ALIGN)
-        late_pairs = keep.tile([P, 2, QUARTER, 2], BF16, name="late_pairs", tag="late_pairs", align_bytes=ALIGN)
-        nc.vector.memset(pairs[:, 1, 2 * QUARTER :, :], 0.0)
 
         def entries(lo, hi):
             return offs_sb[:, lo // 16 : hi // 16]
 
-        def gather_first_word(j):
-            rounded = keep.tile([P, T], BF16, name=f"rounded{j}", tag=f"rounded{j}", align_bytes=ALIGN)
-            nc.scalar.copy(rounded[:, 0:SCALAR_ROUNDS], planes[j][:, 0:SCALAR_ROUNDS])
-            nc.gpsimd.tensor_copy(rounded[:, SCALAR_ROUNDS:], planes[j][:, SCALAR_ROUNDS:])
-            nc.vector.tensor_copy(pairs[:, 0, :, j], planes[j][:].indirect(entries(0, 3 * QUARTER)))
-            nc.scalar.activation(late_pairs[:, 0, :, j], rounded[:].indirect(entries(3 * QUARTER, S)), COPY)
-
-        nc.vector.tensor_copy(pairs[:, 1, :, 0], planes[2][:].indirect(entries(0, 3 * QUARTER)))
-        nc.vector.tensor_copy(late_pairs[:, 1, :, 0], planes[2][:].indirect(entries(3 * QUARTER, S)))
-        gather_first_word(0)
-        gather_first_word(1)
-
-        gate_sb = keep.tile([P, D, V], F32, name="gate_sb", tag="rounded0", align_bytes=ALIGN)
-        nc.scalar.dma_start(gate_sb[:], gate[:, 0:P, :].rearrange("d p v -> p d v"))
-
+        pairs = [keep.tile([P, 2, QUARTER, 2], BF16, name=f"pairs{c}", align_bytes=ALIGN) for c in range(2)]
+        rows = [keep.tile([P, 2, HALF], BF16, name=f"rows{u}", align_bytes=ALIGN) for u in range(2)]
         quads = keep.tile([P, S, 2, 2], BF16, name="quads", align_bytes=ALIGN)
 
-        def weave(source, first, lo, hi, copy=nc.scalar.copy, word=F32):
-            source_words = source[:].rearrange("p u n e -> p (u n e)").bitcast(word).rearrange("p (u n) -> p n u", u=2)
-            quad_words = quads[:, lo:hi, :, :].rearrange("p n u e -> p (n u e)").bitcast(word).rearrange("p (n u) -> p n u", u=2)
-            copy(quad_words, source_words[:, lo - first : hi - first, :])
+        def lay(u, lo, hi):
+            nc.vector.tensor_copy(quads[:, HALF + lo : HALF + hi, u, :], rows[u][:, :, lo:hi].rearrange("p e n -> p n e"))
 
-        weave(pairs, 0, 2 * QUARTER, 3 * QUARTER)
-        nc.vector.tensor_copy(pairs[:, 1, 0 : 2 * QUARTER, 1], planes[3][:].indirect(entries(0, 2 * QUARTER)))
-        weave(pairs, 0, 0, GPSIMD_WEAVES, nc.gpsimd.tensor_copy, U32)
-        weave(pairs, 0, GPSIMD_WEAVES, QUARTER)
-        weave(pairs, 0, QUARTER, 2 * QUARTER)
-        nc.vector.tensor_copy(late_pairs[:, 1, :, 1], planes[3][:].indirect(entries(3 * QUARTER, S)))
-        weave(late_pairs, 3 * QUARTER, 3 * QUARTER, S)
-        nc.vector.tensor_copy(quads[:, 2 * QUARTER : 3 * QUARTER, 1, 1], planes[3][:].indirect(entries(2 * QUARTER, 3 * QUARTER)))
+        def weave(c):
+            source = pairs[c][:].rearrange("p u n e -> p (u n e)").bitcast(F32).rearrange("p (u n) -> p n u", u=2)
+            target = quads[:, c * QUARTER : (c + 1) * QUARTER, :, :].rearrange("p n u e -> p (n u e)").bitcast(F32)
+            nc.scalar.copy(target.rearrange("p (n u) -> p n u", u=2), source)
 
-        front_codes = keep.tile([P, 2 * QUARTER], U32, name="front_codes", align_bytes=ALIGN)
-        back_codes = keep.tile([P, 2 * QUARTER], U32, name="back_codes", tag="pairs", align_bytes=ALIGN)
+        for j in range(PACK):
+            u, e = divmod(j, 2)
+            for c in range(2):
+                nc.vector.tensor_copy(pairs[c][:, u, :, e], planes[j][:].indirect(entries(c * QUARTER, (c + 1) * QUARTER)))
+            if j < PACK - 1:
+                nc.scalar.activation(rows[u][:, e, :], planes[j][:].indirect(entries(HALF, S)), COPY)
+            else:
+                for c in range(2):
+                    nc.scalar.activation(
+                        rows[u][:, e, c * QUARTER : (c + 1) * QUARTER],
+                        planes[j][:].indirect(entries(HALF + c * QUARTER, HALF + (c + 1) * QUARTER)),
+                        COPY,
+                    )
+            if j == 1:
+                lay(0, 0, HALF)
+        lay(1, 0, QUARTER)
+        lay(1, QUARTER, HALF)
+        weave(0)
+        weave(1)
+
+        x_codes = keep.tile([P, S], U32, name="x_codes", align_bytes=ALIGN)
         x_scale = keep.tile([P, S], U8, name="x_scale", align_bytes=ALIGN)
         y = [keep.tile([P, S], F32, name=f"y{h}", align_bytes=ALIGN) for h in range(ROW_TILES)]
-
-        def codes(c):
-            return (front_codes, back_codes)[c // 2][:, c % 2 * QUARTER : (c % 2 + 1) * QUARTER].bitcast(FP8X4)
 
         def layer(h, c):
             columns = slice(c * QUARTER, (c + 1) * QUARTER)
@@ -110,27 +107,37 @@ def tile_picked_sub_lin_relu_sub_e_kernel(tc, xT, w_words, w_scales, b, gate, of
                 out=bank[:],
                 lhsT=w_codes[:, h * P : (h + 1) * P].bitcast(FP8X4),
                 lhsT_scale=w_scale[:, h * P : (h + 1) * P],
-                rhs=codes(c),
+                rhs=x_codes[:, columns].bitcast(FP8X4),
                 rhs_scale=x_scale[:, columns],
                 start=True,
                 stop=True,
             )
             nc.scalar.activation(y[h][:, columns], bank[:], RELU, bias=bias[:, h, :])
 
-        for c in range(4):
+        order = (2, 0, 3, 1)
+        for c in order:
             nc.vector.quantize_mx(
-                out=codes(c),
+                out=x_codes[:, c * QUARTER : (c + 1) * QUARTER].bitcast(FP8X4),
                 scales=x_scale[:, c * QUARTER : (c + 1) * QUARTER],
                 in_=quads[:, c * QUARTER : (c + 1) * QUARTER, :, :].rearrange("p n u e -> p (n u e)"),
             )
             layer(0, c)
-        for c in range(4):
+        for c in order:
             layer(1, c)
 
-        terms = keep.tile([P, D, ROW_TILES, V], F32, name="terms", align_bytes=ALIGN)
-        for h in range(ROW_TILES):
-            for d in range(D):
-                nc.vector.tensor_tensor(terms[:, d, h, :], y[h][:].indirect(pos_sb[d][:]), gate_sb[:, d, :], MULT)
-        for h, queue in enumerate((nc.scalar, nc.sync)):
-            nc.vector.tensor_tensor(terms[:, 0, h, :], terms[:, 0, h, :], terms[:, 1, h, :], ADD)
-            queue.dma_start(out[h * P : (h + 1) * P, :], terms[:, 0, h, :])
+        first = [keep.tile([P, V], F32, name=f"first{h}", align_bytes=ALIGN) for h in range(ROW_TILES)]
+        second = [keep.tile([P, V], F32, name=f"second{h}", align_bytes=ALIGN) for h in range(ROW_TILES)]
+        left, right = slice(0, V // 2), slice(V // 2, V)
+        nc.vector.tensor_tensor(first[0][:], y[0][:].indirect(pos_sb[0][:]), gate_sb[:, 0, :], MULT)
+        nc.scalar.activation(second[0][:], y[0][:].indirect(pos_sb[1][:]), COPY)
+        nc.vector.tensor_tensor(first[1][:], y[1][:].indirect(pos_sb[0][:]), gate_sb[:, 0, :], MULT)
+        nc.scalar.activation(second[1][:, left], y[1][:].indirect(pos_sb[1][:, 0:8]), COPY)
+        nc.scalar.activation(second[1][:, right], y[1][:].indirect(pos_sb[1][:, 8:16]), COPY)
+        nc.vector.tensor_tensor(second[0][:], second[0][:], gate_sb[:, 1, :], MULT)
+        nc.vector.tensor_tensor(second[1][:, left], second[1][:, left], gate_sb[:, 1, left], MULT)
+        nc.vector.tensor_tensor(first[0][:], first[0][:], second[0][:], ADD)
+        nc.sync.dma_start(out[0:P, :], first[0][:])
+        nc.vector.tensor_tensor(second[1][:, right], second[1][:, right], gate_sb[:, 1, right], MULT)
+        nc.vector.tensor_tensor(first[1][:, left], first[1][:, left], second[1][:, left], ADD)
+        nc.vector.tensor_tensor(first[1][:, right], first[1][:, right], second[1][:, right], ADD)
+        nc.sync.dma_start(out[P:N, :], first[1][:])

@@ -23,6 +23,7 @@ ROW_TILES = N // P
 QUARTER = S // 4
 HALF = S // 2
 ALIGN = 256
+FUSED = 64
 
 
 def tile_picked_sub_lin_relu_sub_e_kernel(tc, xT, w_words, w_scales, b, gate, offs, pos1, pos2, out):
@@ -128,12 +129,14 @@ def tile_picked_sub_lin_relu_sub_e_kernel(tc, xT, w_words, w_scales, b, gate, of
         first = [keep.tile([P, V], F32, name=f"first{h}", align_bytes=ALIGN) for h in range(ROW_TILES)]
         second = [keep.tile([P, V], F32, name=f"second{h}", align_bytes=ALIGN) for h in range(ROW_TILES)]
         left, right = slice(0, V // 2), slice(V // 2, V)
+        fused, plain = slice(0, FUSED), slice(FUSED, V)
         nc.vector.tensor_tensor(first[0][:], y[0][:].indirect(pos_sb[0][:]), gate_sb[:, 0, :], MULT)
-        nc.scalar.activation(second[0][:], y[0][:].indirect(pos_sb[1][:]), COPY)
+        nc.vector.tensor_tensor(second[0][:, fused], y[0][:].indirect(pos_sb[1][:, 0 : FUSED // 16]), gate_sb[:, 1, fused], MULT)
+        nc.scalar.activation(second[0][:, plain], y[0][:].indirect(pos_sb[1][:, FUSED // 16 :]), COPY)
         nc.vector.tensor_tensor(first[1][:], y[1][:].indirect(pos_sb[0][:]), gate_sb[:, 0, :], MULT)
         nc.scalar.activation(second[1][:, left], y[1][:].indirect(pos_sb[1][:, 0:8]), COPY)
         nc.scalar.activation(second[1][:, right], y[1][:].indirect(pos_sb[1][:, 8:16]), COPY)
-        nc.vector.tensor_tensor(second[0][:], second[0][:], gate_sb[:, 1, :], MULT)
+        nc.vector.tensor_tensor(second[0][:, plain], second[0][:, plain], gate_sb[:, 1, plain], MULT)
         nc.vector.tensor_tensor(second[1][:, left], second[1][:, left], gate_sb[:, 1, left], MULT)
         nc.vector.tensor_tensor(first[0][:], first[0][:], second[0][:], ADD)
         nc.sync.dma_start(out[0:P, :], first[0][:])

@@ -138,9 +138,8 @@ def tile_picked_sub_lin_relu_sub_e_kernel(tc, xT, w_words, w_scales, b, gate, of
         nc.scalar.activation(second[1][:, right], y[1][:].indirect(pos_sb[1][:, 8:16]), COPY)
         nc.vector.tensor_tensor(second[0][:, plain], second[0][:, plain], gate_sb[:, 1, plain], MULT)
         nc.vector.tensor_tensor(second[1][:, left], second[1][:, left], gate_sb[:, 1, left], MULT)
+        nc.vector.tensor_tensor(second[1][:, right], second[1][:, right], gate_sb[:, 1, right], MULT)
         nc.vector.tensor_tensor(first[0][:], first[0][:], second[0][:], ADD)
         nc.sync.dma_start(out[0:P, :], first[0][:])
-        nc.vector.tensor_tensor(second[1][:, right], second[1][:, right], gate_sb[:, 1, right], MULT)
-        nc.vector.tensor_tensor(first[1][:, left], first[1][:, left], second[1][:, left], ADD)
-        nc.vector.tensor_tensor(first[1][:, right], first[1][:, right], second[1][:, right], ADD)
+        nc.vector.tensor_tensor(first[1][:], first[1][:], second[1][:], ADD)
         nc.sync.dma_start(out[P:N, :], first[1][:])

@@ -70,7 +70,10 @@ def tile_picked_sub_lin_relu_sub_e_kernel(tc, xT, w_words, w_scales, b, gate, of
         quads = keep.tile([P, S, 2, 2], BF16, name="quads", align_bytes=ALIGN)
 
         def lay(u, lo, hi):
-            nc.vector.tensor_copy(quads[:, HALF + lo : HALF + hi, u, :], rows[u][:, :, lo:hi].rearrange("p e n -> p n e"))
+            nc.vector.tensor_copy(
+                quads[:, HALF + lo : HALF + hi, u, :].rearrange("p (c i) e -> p c e i", i=4),
+                rows[u][:, :, lo:hi].rearrange("p e (c i) -> p c e i", i=4),
+            )
 
         def weave(c):
             source = pairs[c][:].rearrange("p u n e -> p (u n e)").bitcast(F32).rearrange("p (u n) -> p n u", u=2)

@@ -24,6 +24,7 @@ QUARTER = S // 4
 HALF = S // 2
 ALIGN = 256
 FUSED = 64
+LEAD = 128
 
 
 def tile_picked_sub_lin_relu_sub_e_kernel(tc, xT, w_words, w_scales, b, gate, offs, pos1, pos2, out):
@@ -65,40 +66,16 @@ def tile_picked_sub_lin_relu_sub_e_kernel(tc, xT, w_words, w_scales, b, gate, of
         def entries(lo, hi):
             return offs_sb[:, lo // 16 : hi // 16]
 
-        pairs = [keep.tile([P, 2, QUARTER, 2], BF16, name=f"pairs{c}", align_bytes=ALIGN) for c in range(2)]
-        rows = [keep.tile([P, 2, HALF], BF16, name=f"rows{u}", align_bytes=ALIGN) for u in range(2)]
+        spans = ((0, LEAD), (3 * QUARTER, S))
+        rows = [[keep.tile([P, 2, hi - lo], BF16, name=f"rows{u}{s}", align_bytes=ALIGN) for s, (lo, hi) in enumerate(spans)] for u in range(2)]
         quads = keep.tile([P, S, 2, 2], BF16, name="quads", align_bytes=ALIGN)
 
-        def lay(u, lo, hi):
+        def lay(u, s):
+            lo, hi = spans[s]
             nc.vector.tensor_copy(
-                quads[:, HALF + lo : HALF + hi, u, :].rearrange("p (c i) e -> p c e i", i=4),
-                rows[u][:, :, lo:hi].rearrange("p e (c i) -> p c e i", i=4),
+                quads[:, lo:hi, u, :].rearrange("p (c i) e -> p c e i", i=4),
+                rows[u][s][:].rearrange("p e (c i) -> p c e i", i=4),
             )
-
-        def weave(c):
-            source = pairs[c][:].rearrange("p u n e -> p (u n e)").bitcast(F32).rearrange("p (u n) -> p n u", u=2)
-            target = quads[:, c * QUARTER : (c + 1) * QUARTER, :, :].rearrange("p n u e -> p (n u e)").bitcast(F32)
-            nc.scalar.copy(target.rearrange("p (n u) -> p n u", u=2), source)
-
-        for j in range(PACK):
-            u, e = divmod(j, 2)
-            for c in range(2):
-                nc.vector.tensor_copy(pairs[c][:, u, :, e], planes[j][:].indirect(entries(c * QUARTER, (c + 1) * QUARTER)))
-            if j < PACK - 1:
-                nc.scalar.activation(rows[u][:, e, :], planes[j][:].indirect(entries(HALF, S)), COPY)
-            else:
-                for c in range(2):
-                    nc.scalar.activation(
-                        rows[u][:, e, c * QUARTER : (c + 1) * QUARTER],
-                        planes[j][:].indirect(entries(HALF + c * QUARTER, HALF + (c + 1) * QUARTER)),
-                        COPY,
-                    )
-            if j == 1:
-                lay(0, 0, HALF)
-        lay(1, 0, QUARTER)
-        lay(1, QUARTER, HALF)
-        weave(0)
-        weave(1)
 
         x_codes = keep.tile([P, S], U32, name="x_codes", align_bytes=ALIGN)
         x_scale = keep.tile([P, S], U8, name="x_scale", align_bytes=ALIGN)
@@ -118,15 +95,30 @@ def tile_picked_sub_lin_relu_sub_e_kernel(tc, xT, w_words, w_scales, b, gate, of
             )
             nc.scalar.activation(y[h][:, columns], bank[:], RELU, bias=bias[:, h, :])
 
-        order = (2, 0, 3, 1)
-        for c in order:
+        def quantise(c):
             nc.vector.quantize_mx(
                 out=x_codes[:, c * QUARTER : (c + 1) * QUARTER].bitcast(FP8X4),
                 scales=x_scale[:, c * QUARTER : (c + 1) * QUARTER],
                 in_=quads[:, c * QUARTER : (c + 1) * QUARTER, :, :].rearrange("p n u e -> p (n u e)"),
             )
             layer(0, c)
-        for c in order:
+
+        for j in range(PACK):
+            u, e = divmod(j, 2)
+            for lo, hi in ((HALF, 3 * QUARTER), (LEAD, HALF)):
+                nc.vector.tensor_copy(quads[:, lo:hi, u, e], planes[j][:].indirect(entries(lo, hi)))
+            for s, (lo, hi) in enumerate(spans):
+                nc.scalar.activation(rows[u][s][:, e, :], planes[j][:].indirect(entries(lo, hi)), COPY)
+            if j == 1:
+                lay(0, 0)
+                lay(0, 1)
+        lay(1, 0)
+        quantise(2)
+        layer(1, 2)
+        lay(1, 1)
+        for c in (1, 0, 3):
+            quantise(c)
+        for c in (1, 0, 3):
             layer(1, c)
 
         first = [keep.tile([P, V], F32, name=f"first{h}", align_bytes=ALIGN) for h in range(ROW_TILES)]

@@ -16,6 +16,7 @@ RELU = mybir.ActivationFunctionType.Relu
 COPY = mybir.ActivationFunctionType.Copy
 MULT = mybir.AluOpType.mult
 ADD = mybir.AluOpType.add
+MAX = mybir.AluOpType.max
 
 P = 128
 PACK = 4
@@ -23,8 +24,8 @@ ROW_TILES = N // P
 QUARTER = S // 4
 HALF = S // 2
 ALIGN = 256
-FUSED = 64
 LEAD = 128
+SHARE = 64
 
 
 def tile_picked_sub_lin_relu_sub_e_kernel(tc, xT, w_words, w_scales, b, gate, offs, pos1, pos2, out):
@@ -70,11 +71,10 @@ def tile_picked_sub_lin_relu_sub_e_kernel(tc, xT, w_words, w_scales, b, gate, of
         rows = [[keep.tile([P, 2, hi - lo], BF16, name=f"rows{u}{s}", align_bytes=ALIGN) for s, (lo, hi) in enumerate(spans)] for u in range(2)]
         quads = keep.tile([P, S, 2, 2], BF16, name="quads", align_bytes=ALIGN)
 
-        def lay(u, s):
-            lo, hi = spans[s]
-            nc.vector.tensor_copy(
-                quads[:, lo:hi, u, :].rearrange("p (c i) e -> p c e i", i=4),
-                rows[u][s][:].rearrange("p e (c i) -> p c e i", i=4),
+        def lay(copy, u, s, lo, hi):
+            copy(
+                quads[:, spans[s][0] + lo : spans[s][0] + hi, u, :].rearrange("p (c i) e -> p c e i", i=4),
+                rows[u][s][:, :, lo:hi].rearrange("p e (c i) -> p c e i", i=4),
             )
 
         x_codes = keep.tile([P, S], U32, name="x_codes", align_bytes=ALIGN)
@@ -93,7 +93,10 @@ def tile_picked_sub_lin_relu_sub_e_kernel(tc, xT, w_words, w_scales, b, gate, of
                 start=True,
                 stop=True,
             )
-            nc.scalar.activation(y[h][:, columns], bank[:], RELU, bias=bias[:, h, :])
+            if (h, c) == (1, 1):
+                nc.vector.tensor_scalar(y[h][:, columns], bank[:], bias[:, h, :], 0.0, ADD, MAX)
+            else:
+                nc.scalar.activation(y[h][:, columns], bank[:], RELU, bias=bias[:, h, :])
 
         def quantise(c):
             nc.vector.quantize_mx(
@@ -110,12 +113,13 @@ def tile_picked_sub_lin_relu_sub_e_kernel(tc, xT, w_words, w_scales, b, gate, of
             for s, (lo, hi) in enumerate(spans):
                 nc.scalar.activation(rows[u][s][:, e, :], planes[j][:].indirect(entries(lo, hi)), COPY)
             if j == 1:
-                lay(0, 0)
-                lay(0, 1)
-        lay(1, 0)
+                lay(nc.vector.tensor_copy, 0, 0, 0, QUARTER)
+                lay(nc.vector.tensor_copy, 0, 1, 0, QUARTER)
+        lay(nc.scalar.copy, 1, 0, SHARE, QUARTER)
+        lay(nc.vector.tensor_copy, 1, 0, 0, SHARE)
         quantise(2)
         layer(1, 2)
-        lay(1, 1)
+        lay(nc.vector.tensor_copy, 1, 1, 0, QUARTER)
         for c in (1, 0, 3):
             quantise(c)
         for c in (1, 0, 3):
@@ -124,17 +128,15 @@ def tile_picked_sub_lin_relu_sub_e_kernel(tc, xT, w_words, w_scales, b, gate, of
         first = [keep.tile([P, V], F32, name=f"first{h}", align_bytes=ALIGN) for h in range(ROW_TILES)]
         second = [keep.tile([P, V], F32, name=f"second{h}", align_bytes=ALIGN) for h in range(ROW_TILES)]
         left, right = slice(0, V // 2), slice(V // 2, V)
-        fused, plain = slice(0, FUSED), slice(FUSED, V)
         nc.vector.tensor_tensor(first[0][:], y[0][:].indirect(pos_sb[0][:]), gate_sb[:, 0, :], MULT)
-        nc.vector.tensor_tensor(second[0][:, fused], y[0][:].indirect(pos_sb[1][:, 0 : FUSED // 16]), gate_sb[:, 1, fused], MULT)
-        nc.scalar.activation(second[0][:, plain], y[0][:].indirect(pos_sb[1][:, FUSED // 16 :]), COPY)
+        nc.scalar.activation(second[0][:], y[0][:].indirect(pos_sb[1][:]), COPY)
         nc.vector.tensor_tensor(first[1][:], y[1][:].indirect(pos_sb[0][:]), gate_sb[:, 0, :], MULT)
         nc.scalar.activation(second[1][:, left], y[1][:].indirect(pos_sb[1][:, 0:8]), COPY)
         nc.scalar.activation(second[1][:, right], y[1][:].indirect(pos_sb[1][:, 8:16]), COPY)
-        nc.vector.tensor_tensor(second[0][:, plain], second[0][:, plain], gate_sb[:, 1, plain], MULT)
+        nc.vector.tensor_tensor(second[0][:], second[0][:], gate_sb[:, 1, :], MULT)
         nc.vector.tensor_tensor(second[1][:, left], second[1][:, left], gate_sb[:, 1, left], MULT)
-        nc.vector.tensor_tensor(second[1][:, right], second[1][:, right], gate_sb[:, 1, right], MULT)
         nc.vector.tensor_tensor(first[0][:], first[0][:], second[0][:], ADD)
+        nc.vector.tensor_tensor(second[1][:, right], second[1][:, right], gate_sb[:, 1, right], MULT)
         nc.sync.dma_start(out[0:P, :], first[0][:])
         nc.vector.tensor_tensor(first[1][:], first[1][:], second[1][:], ADD)
         nc.sync.dma_start(out[P:N, :], first[1][:])

@@ -26,6 +26,7 @@ HALF = S // 2
 ALIGN = 256
 LEAD = 128
 SHARE = 64
+CUT = 192
 
 
 def tile_picked_sub_lin_relu_sub_e_kernel(tc, xT, w_words, w_scales, b, gate, offs, pos1, pos2, out):
@@ -127,16 +128,16 @@ def tile_picked_sub_lin_relu_sub_e_kernel(tc, xT, w_words, w_scales, b, gate, of
 
         first = [keep.tile([P, V], F32, name=f"first{h}", align_bytes=ALIGN) for h in range(ROW_TILES)]
         second = [keep.tile([P, V], F32, name=f"second{h}", align_bytes=ALIGN) for h in range(ROW_TILES)]
-        left, right = slice(0, V // 2), slice(V // 2, V)
+        left, right = slice(0, CUT), slice(CUT, V)
         nc.vector.tensor_tensor(first[0][:], y[0][:].indirect(pos_sb[0][:]), gate_sb[:, 0, :], MULT)
         nc.scalar.activation(second[0][:], y[0][:].indirect(pos_sb[1][:]), COPY)
         nc.vector.tensor_tensor(first[1][:], y[1][:].indirect(pos_sb[0][:]), gate_sb[:, 0, :], MULT)
-        nc.scalar.activation(second[1][:, left], y[1][:].indirect(pos_sb[1][:, 0:8]), COPY)
-        nc.scalar.activation(second[1][:, right], y[1][:].indirect(pos_sb[1][:, 8:16]), COPY)
+        nc.scalar.activation(second[1][:, left], y[1][:].indirect(pos_sb[1][:, 0 : CUT // 16]), COPY)
+        nc.scalar.activation(second[1][:, right], y[1][:].indirect(pos_sb[1][:, CUT // 16 :]), COPY)
         nc.vector.tensor_tensor(second[0][:], second[0][:], gate_sb[:, 1, :], MULT)
         nc.vector.tensor_tensor(second[1][:, left], second[1][:, left], gate_sb[:, 1, left], MULT)
-        nc.vector.tensor_tensor(first[0][:], first[0][:], second[0][:], ADD)
         nc.vector.tensor_tensor(second[1][:, right], second[1][:, right], gate_sb[:, 1, right], MULT)
+        nc.vector.tensor_tensor(first[0][:], first[0][:], second[0][:], ADD)
         nc.sync.dma_start(out[0:P, :], first[0][:])
         nc.vector.tensor_tensor(first[1][:], first[1][:], second[1][:], ADD)
         nc.sync.dma_start(out[P:N, :], first[1][:])

@@ -120,7 +120,8 @@ def tile_picked_sub_lin_relu_sub_e_kernel(tc, xT, w_words, w_scales, b, gate, of
         lay(nc.vector.tensor_copy, 1, 0, 0, SHARE)
         quantise(2)
         layer(1, 2)
-        lay(nc.vector.tensor_copy, 1, 1, 0, QUARTER)
+        lay(nc.scalar.copy, 1, 1, 96, QUARTER)
+        lay(nc.vector.tensor_copy, 1, 1, 0, 96)
         for c in (1, 0, 3):
             quantise(c)
         for c in (1, 0, 3):

@@ -61,8 +61,8 @@ def tile_picked_sub_lin_relu_sub_e_kernel(tc, xT, w_words, w_scales, b, gate, of
         nc.sync.dma_start(w_codes[:].bitcast(I32), w_words[0].rearrange("p n r -> p (n r)").bitcast(I32))
         with nc.allow_non_contiguous_dma(reason="one bias value a partition"):
             nc.sync.dma_start(bias[:], b.rearrange("(h p) o -> p h o", p=P))
-        nc.sync.dma_start(gate_sb[:], gate[:, 0:P, :].rearrange("d p v -> p d v"))
         nc.sync.dma_start(pos_sb[0][:], pos1)
+        nc.sync.dma_start(gate_sb[:], gate[:, 0:P, :].rearrange("d p v -> p d v"))
         nc.sync.dma_start(pos_sb[1][:], pos2)
 
         def entries(lo, hi):

@@ -114,7 +114,7 @@ def tile_picked_sub_lin_relu_sub_e_kernel(tc, xT, w_words, w_scales, b, gate, of
             for s, (lo, hi) in enumerate(spans):
                 nc.scalar.activation(rows[u][s][:, e, :], planes[j][:].indirect(entries(lo, hi)), COPY)
             if j == 1:
-                lay(nc.vector.tensor_copy, 0, 0, 0, QUARTER)
+                lay(nc.scalar.copy, 0, 0, 0, QUARTER)
                 lay(nc.vector.tensor_copy, 0, 1, 0, QUARTER)
         lay(nc.scalar.copy, 1, 0, SHARE, QUARTER)
         lay(nc.vector.tensor_copy, 1, 0, 0, SHARE)

@@ -120,8 +120,8 @@ def tile_picked_sub_lin_relu_sub_e_kernel(tc, xT, w_words, w_scales, b, gate, of
         lay(nc.vector.tensor_copy, 1, 0, 0, SHARE)
         quantise(2)
         layer(1, 2)
-        lay(nc.scalar.copy, 1, 1, 96, QUARTER)
-        lay(nc.vector.tensor_copy, 1, 1, 0, 96)
+        lay(nc.scalar.copy, 1, 1, 32, QUARTER)
+        lay(nc.vector.tensor_copy, 1, 1, 0, 32)
         for c in (1, 0, 3):
             quantise(c)
         for c in (1, 0, 3):

@@ -22,9 +22,7 @@ P = 128
 PACK = 4
 ROW_TILES = N // P
 QUARTER = S // 4
-HALF = S // 2
 ALIGN = 256
-LEAD = 128
 SHARE = 64
 CUT = 192
 
@@ -68,14 +66,15 @@ def tile_picked_sub_lin_relu_sub_e_kernel(tc, xT, w_words, w_scales, b, gate, of
         def entries(lo, hi):
             return offs_sb[:, lo // 16 : hi // 16]
 
-        spans = ((0, LEAD), (3 * QUARTER, S))
+        placed = ((0, QUARTER), (QUARTER + SHARE, 2 * QUARTER + SHARE))
+        spans = ((QUARTER, QUARTER + SHARE), (2 * QUARTER + SHARE, S))
         rows = [[keep.tile([P, 2, hi - lo], BF16, name=f"rows{u}{s}", align_bytes=ALIGN) for s, (lo, hi) in enumerate(spans)] for u in range(2)]
         quads = keep.tile([P, S, 2, 2], BF16, name="quads", align_bytes=ALIGN)
 
         def lay(copy, u, s, lo, hi):
             copy(
-                quads[:, spans[s][0] + lo : spans[s][0] + hi, u, :].rearrange("p (c i) e -> p c e i", i=4),
-                rows[u][s][:, :, lo:hi].rearrange("p e (c i) -> p c e i", i=4),
+                quads[:, lo:hi, u, :].rearrange("p (c i) e -> p c e i", i=4),
+                rows[u][s][:, :, lo - spans[s][0] : hi - spans[s][0]].rearrange("p e (c i) -> p c e i", i=4),
             )
 
         x_codes = keep.tile([P, S], U32, name="x_codes", align_bytes=ALIGN)
@@ -109,22 +108,22 @@ def tile_picked_sub_lin_relu_sub_e_kernel(tc, xT, w_words, w_scales, b, gate, of
 
         for j in range(PACK):
             u, e = divmod(j, 2)
-            for lo, hi in ((HALF, 3 * QUARTER), (LEAD, HALF)):
+            for lo, hi in placed:
                 nc.vector.tensor_copy(quads[:, lo:hi, u, e], planes[j][:].indirect(entries(lo, hi)))
             for s, (lo, hi) in enumerate(spans):
                 nc.scalar.activation(rows[u][s][:, e, :], planes[j][:].indirect(entries(lo, hi)), COPY)
             if j == 1:
-                lay(nc.scalar.copy, 0, 0, 0, QUARTER)
-                lay(nc.vector.tensor_copy, 0, 1, 0, QUARTER)
-        lay(nc.scalar.copy, 1, 0, SHARE, QUARTER)
-        lay(nc.vector.tensor_copy, 1, 0, 0, SHARE)
-        quantise(2)
-        layer(1, 2)
-        lay(nc.scalar.copy, 1, 1, 32, QUARTER)
-        lay(nc.vector.tensor_copy, 1, 1, 0, 32)
-        for c in (1, 0, 3):
+                lay(nc.scalar.copy, 0, 0, *spans[0])
+                lay(nc.vector.tensor_copy, 0, 1, *spans[1])
+        quantise(0)
+        layer(1, 0)
+        lay(nc.scalar.copy, 1, 0, *spans[0])
+        lay(nc.vector.tensor_copy, 1, 1, spans[1][0], 3 * QUARTER)
+        lay(nc.vector.tensor_copy, 1, 1, 3 * QUARTER, S - SHARE)
+        lay(nc.scalar.copy, 1, 1, S - SHARE, S)
+        for c in (1, 2, 3):
             quantise(c)
-        for c in (1, 0, 3):
+        for c in (1, 2, 3):
             layer(1, c)
 
         first = [keep.tile([P, V], F32, name=f"first{h}", align_bytes=ALIGN) for h in range(ROW_TILES)]

@@ -67,25 +67,29 @@ def tile_picked_sub_lin_relu_sub_e_kernel(tc, xT, w_words, w_scales, b, gate, of
             return offs_sb[:, lo // 16 : hi // 16]
 
         placed = ((0, QUARTER), (QUARTER + SHARE, 2 * QUARTER + SHARE))
-        spans = ((QUARTER, QUARTER + SHARE), (2 * QUARTER + SHARE, S))
-        rows = [[keep.tile([P, 2, hi - lo], BF16, name=f"rows{u}{s}", align_bytes=ALIGN) for s, (lo, hi) in enumerate(spans)] for u in range(2)]
+        spans = ((QUARTER, QUARTER + SHARE), (2 * QUARTER + SHARE, 3 * QUARTER), (3 * QUARTER, S))
+        rows = [keep.tile([P, 2, S], BF16, name=f"rows{u}", align_bytes=ALIGN) for u in range(2)]
         quads = keep.tile([P, S, 2, 2], BF16, name="quads", align_bytes=ALIGN)
 
-        def lay(copy, u, s, lo, hi):
+        def fetch(j, lo, hi):
+            nc.scalar.activation(rows[j // 2][:, j % 2, lo:hi], planes[j][:].indirect(entries(lo, hi)), COPY)
+
+        def lay(copy, u, lo, hi):
             copy(
                 quads[:, lo:hi, u, :].rearrange("p (c i) e -> p c e i", i=4),
-                rows[u][s][:, :, lo - spans[s][0] : hi - spans[s][0]].rearrange("p e (c i) -> p c e i", i=4),
+                rows[u][:, :, lo:hi].rearrange("p e (c i) -> p c e i", i=4),
             )
 
         x_codes = keep.tile([P, S], U32, name="x_codes", align_bytes=ALIGN)
         x_scale = keep.tile([P, S], U8, name="x_scale", align_bytes=ALIGN)
         y = [keep.tile([P, S], F32, name=f"y{h}", align_bytes=ALIGN) for h in range(ROW_TILES)]
 
-        def layer(h, c):
+        banks = [[psum.tile([P, QUARTER], F32, name=f"bank{h}{c}") for c in range(4)] for h in range(ROW_TILES)]
+
+        def multiply(h, c):
             columns = slice(c * QUARTER, (c + 1) * QUARTER)
-            bank = psum.tile([P, QUARTER], F32, name=f"bank{h}{c}")
             nc.tensor.matmul_mx(
-                out=bank[:],
+                out=banks[h][c][:],
                 lhsT=w_codes[:, h * P : (h + 1) * P].bitcast(FP8X4),
                 lhsT_scale=w_scale[:, h * P : (h + 1) * P],
                 rhs=x_codes[:, columns].bitcast(FP8X4),
@@ -93,37 +97,54 @@ def tile_picked_sub_lin_relu_sub_e_kernel(tc, xT, w_words, w_scales, b, gate, of
                 start=True,
                 stop=True,
             )
-            if (h, c) == (1, 1):
-                nc.vector.tensor_scalar(y[h][:, columns], bank[:], bias[:, h, :], 0.0, ADD, MAX)
-            else:
-                nc.scalar.activation(y[h][:, columns], bank[:], RELU, bias=bias[:, h, :])
 
-        def quantise(c):
+        def rectify(h, c):
+            columns = slice(c * QUARTER, (c + 1) * QUARTER)
+            if (h, c) == (1, 1):
+                nc.vector.tensor_scalar(y[h][:, columns], banks[h][c][:], bias[:, h, :], 0.0, ADD, MAX)
+            else:
+                nc.scalar.activation(y[h][:, columns], banks[h][c][:], RELU, bias=bias[:, h, :])
+
+        def layer(h, c):
+            multiply(h, c)
+            rectify(h, c)
+
+        def quantise(lo, hi):
             nc.vector.quantize_mx(
-                out=x_codes[:, c * QUARTER : (c + 1) * QUARTER].bitcast(FP8X4),
-                scales=x_scale[:, c * QUARTER : (c + 1) * QUARTER],
-                in_=quads[:, c * QUARTER : (c + 1) * QUARTER, :, :].rearrange("p n u e -> p (n u e)"),
+                out=x_codes[:, lo:hi].bitcast(FP8X4),
+                scales=x_scale[:, lo:hi],
+                in_=quads[:, lo:hi, :, :].rearrange("p n u e -> p (n u e)"),
             )
-            layer(0, c)
 
         for j in range(PACK):
             u, e = divmod(j, 2)
             for lo, hi in placed:
                 nc.vector.tensor_copy(quads[:, lo:hi, u, e], planes[j][:].indirect(entries(lo, hi)))
-            for s, (lo, hi) in enumerate(spans):
-                nc.scalar.activation(rows[u][s][:, e, :], planes[j][:].indirect(entries(lo, hi)), COPY)
+            fetch(j, *spans[0])
+            if j < PACK - 1:
+                fetch(j, spans[1][0], S)
             if j == 1:
-                lay(nc.scalar.copy, 0, 0, *spans[0])
-                lay(nc.vector.tensor_copy, 0, 1, *spans[1])
-        quantise(0)
+                lay(nc.scalar.copy, 0, *spans[0])
+                lay(nc.vector.tensor_copy, 0, spans[1][0], S)
+        fetch(PACK - 1, *spans[1])
+        lay(nc.scalar.copy, 1, *spans[0])
+        fetch(PACK - 1, *spans[2])
+        lay(nc.scalar.copy, 1, 3 * QUARTER, S - SHARE)
+        quantise(0, QUARTER)
+        layer(0, 0)
         layer(1, 0)
-        lay(nc.scalar.copy, 1, 0, *spans[0])
-        lay(nc.vector.tensor_copy, 1, 1, spans[1][0], 3 * QUARTER)
-        lay(nc.vector.tensor_copy, 1, 1, 3 * QUARTER, S - SHARE)
-        lay(nc.scalar.copy, 1, 1, S - SHARE, S)
-        for c in (1, 2, 3):
-            quantise(c)
-        for c in (1, 2, 3):
+        lay(nc.vector.tensor_copy, 1, *spans[1])
+        quantise(QUARTER, 2 * QUARTER)
+        layer(0, 1)
+        multiply(1, 1)
+        lay(nc.vector.tensor_copy, 1, S - SHARE, S)
+        quantise(2 * QUARTER, 3 * QUARTER)
+        layer(0, 2)
+        quantise(3 * QUARTER, S - SHARE)
+        quantise(S - SHARE, S)
+        layer(0, 3)
+        rectify(1, 1)
+        for c in (2, 3):
             layer(1, c)
 
         first = [keep.tile([P, V], F32, name=f"first{h}", align_bytes=ALIGN) for h in range(ROW_TILES)]

@@ -136,15 +136,13 @@ def tile_picked_sub_lin_relu_sub_e_kernel(tc, xT, w_words, w_scales, b, gate, of
         lay(nc.vector.tensor_copy, 1, *spans[1])
         quantise(QUARTER, 2 * QUARTER)
         layer(0, 1)
-        multiply(1, 1)
         lay(nc.vector.tensor_copy, 1, S - SHARE, S)
         quantise(2 * QUARTER, 3 * QUARTER)
         layer(0, 2)
         quantise(3 * QUARTER, S - SHARE)
         quantise(S - SHARE, S)
         layer(0, 3)
-        rectify(1, 1)
-        for c in (2, 3):
+        for c in (1, 2, 3):
             layer(1, c)
 
         first = [keep.tile([P, V], F32, name=f"first{h}", align_bytes=ALIGN) for h in range(ROW_TILES)]

from contextlib import ExitStack

import concourse.mybir as mybir

K, T, S, V, N, D = 512, 1024, 512, 256, 256, 2
FLOPS = 2 * K * N * S

F32 = mybir.dt.float32
BF16 = mybir.dt.bfloat16
I32 = mybir.dt.int32
U32 = mybir.dt.uint32
U16 = mybir.dt.uint16
U8 = mybir.dt.uint8
FP8X4 = mybir.dt.float8_e4m3fn_x4
RELU = mybir.ActivationFunctionType.Relu
COPY = mybir.ActivationFunctionType.Copy
MULT = mybir.AluOpType.mult
ADD = mybir.AluOpType.add
MAX = mybir.AluOpType.max

P = 128
PACK = 4
ROW_TILES = N // P
QUARTER = S // 4
ALIGN = 256
SHARE = 64
CUT = 192


def tile_picked_sub_lin_relu_sub_e_kernel(tc, xT, w_words, w_scales, b, gate, offs, pos1, pos2, out):
    nc = tc.nc
    with ExitStack() as ctx:
        keep = ctx.enter_context(tc.tile_pool(name="keep", bufs=1))
        psum = ctx.enter_context(tc.psum_pool(name="psum", bufs=1))

        offs_sb = keep.tile([P, S // 16], U16, name="offs_sb")
        pos_sb = [keep.tile([P, V // 16], U16, name=f"pos_sb{d}") for d in range(D)]
        planes = [keep.tile([P, T], F32, name=f"plane{j}", align_bytes=ALIGN) for j in range(PACK)]
        w_codes = keep.tile([P, N], U32, name="w_codes", align_bytes=ALIGN)
        w_scale = keep.tile([P, N], U8, name="w_scale", align_bytes=ALIGN)
        bias = keep.tile([P, ROW_TILES, 1], F32, name="bias")
        gate_sb = keep.tile([P, D, V], F32, name="gate_sb", align_bytes=ALIGN)

        nc.vector.memset(w_scale[:].bitcast(I32), 0)
        warm = keep.tile([P, 2], F32, name="warm")
        nc.vector.memset(warm[:, 0:1], 0.0)
        nc.scalar.copy(warm[:, 1:2], warm[:, 0:1])

        x_rows = xT.rearrange("(p j) t -> p j t", j=PACK)
        nc.sync.dma_start(planes[0][:], x_rows[:, 0, :])
        nc.sync.dma_start(offs_sb[:], offs)
        for j in (1, 2, 3):
            nc.sync.dma_start(planes[j][:], x_rows[:, j, :])
        for quadrant in range(4):
            nc.sync.dma_start(
                w_scale[32 * quadrant : 32 * quadrant + 4, :].bitcast(I32),
                w_scales[0, 4 * quadrant : 4 * quadrant + 4, :].bitcast(I32),
            )
        nc.sync.dma_start(w_codes[:].bitcast(I32), w_words[0].rearrange("p n r -> p (n r)").bitcast(I32))
        with nc.allow_non_contiguous_dma(reason="one bias value a partition"):
            nc.sync.dma_start(bias[:], b.rearrange("(h p) o -> p h o", p=P))
        nc.sync.dma_start(pos_sb[0][:], pos1)
        nc.sync.dma_start(gate_sb[:], gate[:, 0:P, :].rearrange("d p v -> p d v"))
        nc.sync.dma_start(pos_sb[1][:], pos2)

        def entries(lo, hi):
            return offs_sb[:, lo // 16 : hi // 16]

        placed = ((0, QUARTER), (QUARTER + SHARE, 2 * QUARTER + SHARE))
        spans = ((QUARTER, QUARTER + SHARE), (2 * QUARTER + SHARE, 3 * QUARTER), (3 * QUARTER, S))
        rows = [keep.tile([P, 2, S], BF16, name=f"rows{u}", align_bytes=ALIGN) for u in range(2)]
        quads = keep.tile([P, S, 2, 2], BF16, name="quads", align_bytes=ALIGN)

        def fetch(j, lo, hi):
            nc.scalar.activation(rows[j // 2][:, j % 2, lo:hi], planes[j][:].indirect(entries(lo, hi)), COPY)

        def lay(copy, u, lo, hi):
            copy(
                quads[:, lo:hi, u, :].rearrange("p (c i) e -> p c e i", i=4),
                rows[u][:, :, lo:hi].rearrange("p e (c i) -> p c e i", i=4),
            )

        x_codes = keep.tile([P, S], U32, name="x_codes", align_bytes=ALIGN)
        x_scale = keep.tile([P, S], U8, name="x_scale", align_bytes=ALIGN)
        y = [keep.tile([P, S], F32, name=f"y{h}", align_bytes=ALIGN) for h in range(ROW_TILES)]

        banks = [[psum.tile([P, QUARTER], F32, name=f"bank{h}{c}") for c in range(4)] for h in range(ROW_TILES)]

        def multiply(h, c):
            columns = slice(c * QUARTER, (c + 1) * QUARTER)
            nc.tensor.matmul_mx(
                out=banks[h][c][:],
                lhsT=w_codes[:, h * P : (h + 1) * P].bitcast(FP8X4),
                lhsT_scale=w_scale[:, h * P : (h + 1) * P],
                rhs=x_codes[:, columns].bitcast(FP8X4),
                rhs_scale=x_scale[:, columns],
                start=True,
                stop=True,
            )

        def rectify(h, c):
            columns = slice(c * QUARTER, (c + 1) * QUARTER)
            if (h, c) == (1, 1):
                nc.vector.tensor_scalar(y[h][:, columns], banks[h][c][:], bias[:, h, :], 0.0, ADD, MAX)
            else:
                nc.scalar.activation(y[h][:, columns], banks[h][c][:], RELU, bias=bias[:, h, :])

        def layer(h, c):
            multiply(h, c)
            rectify(h, c)

        def quantise(lo, hi):
            nc.vector.quantize_mx(
                out=x_codes[:, lo:hi].bitcast(FP8X4),
                scales=x_scale[:, lo:hi],
                in_=quads[:, lo:hi, :, :].rearrange("p n u e -> p (n u e)"),
            )

        for j in range(PACK):
            u, e = divmod(j, 2)
            for lo, hi in placed:
                nc.vector.tensor_copy(quads[:, lo:hi, u, e], planes[j][:].indirect(entries(lo, hi)))
            fetch(j, *spans[0])
            if j < PACK - 1:
                fetch(j, spans[1][0], S)
            if j == 1:
                lay(nc.scalar.copy, 0, *spans[0])
                lay(nc.vector.tensor_copy, 0, spans[1][0], S)
        fetch(PACK - 1, *spans[1])
        lay(nc.scalar.copy, 1, *spans[0])
        fetch(PACK - 1, *spans[2])
        lay(nc.scalar.copy, 1, 3 * QUARTER, S - SHARE)
        quantise(0, QUARTER)
        layer(0, 0)
        layer(1, 0)
        lay(nc.vector.tensor_copy, 1, *spans[1])
        quantise(QUARTER, 2 * QUARTER)
        layer(0, 1)
        lay(nc.vector.tensor_copy, 1, S - SHARE, S)
        quantise(2 * QUARTER, 3 * QUARTER)
        layer(0, 2)
        quantise(3 * QUARTER, S - SHARE)
        quantise(S - SHARE, S)
        layer(0, 3)
        for c in (1, 2, 3):
            layer(1, c)

        first = [keep.tile([P, V], F32, name=f"first{h}", align_bytes=ALIGN) for h in range(ROW_TILES)]
        second = [keep.tile([P, V], F32, name=f"second{h}", align_bytes=ALIGN) for h in range(ROW_TILES)]
        left, right = slice(0, CUT), slice(CUT, V)
        nc.vector.tensor_tensor(first[0][:], y[0][:].indirect(pos_sb[0][:]), gate_sb[:, 0, :], MULT)
        nc.scalar.activation(second[0][:], y[0][:].indirect(pos_sb[1][:]), COPY)
        nc.vector.tensor_tensor(first[1][:], y[1][:].indirect(pos_sb[0][:]), gate_sb[:, 0, :], MULT)
        nc.scalar.activation(second[1][:, left], y[1][:].indirect(pos_sb[1][:, 0 : CUT // 16]), COPY)
        nc.scalar.activation(second[1][:, right], y[1][:].indirect(pos_sb[1][:, CUT // 16 :]), COPY)
        nc.vector.tensor_tensor(second[0][:], second[0][:], gate_sb[:, 1, :], MULT)
        nc.vector.tensor_tensor(second[1][:, left], second[1][:, left], gate_sb[:, 1, left], MULT)
        nc.vector.tensor_tensor(second[1][:, right], second[1][:, right], gate_sb[:, 1, right], MULT)
        nc.vector.tensor_tensor(first[0][:], first[0][:], second[0][:], ADD)
        nc.sync.dma_start(out[0:P, :], first[0][:])
        nc.vector.tensor_tensor(first[1][:], first[1][:], second[1][:], ADD)
        nc.sync.dma_start(out[P:N, :], first[1][:])
